import numpy as np
import ml_dtypes


def mxq(x, axis, fmt="e4m3"):
    dtype, down = {"e4m3": (ml_dtypes.float8_e4m3fn, 7), "e5m2": (ml_dtypes.float8_e5m2, 14)}[fmt]
    v = np.moveaxis(np.asarray(x, np.float32).astype(ml_dtypes.bfloat16).astype(np.float64), axis, -1)
    blocks = v.reshape(v.shape[:-1] + (-1, 32))
    amax = np.abs(blocks).max(-1, keepdims=True)
    byte = np.maximum(np.where(amax > 0, np.frexp(amax)[1] - 1 + 127, 0) - down, 1)
    scale = np.exp2(byte - 127.0)
    codes = (blocks / scale).astype(np.float32).astype(dtype).astype(np.float64)
    return np.moveaxis((codes * scale).reshape(v.shape), -1, axis)


WIDE = False


def mx_kscale(k):
    if not WIDE:
        return np.ones(k)
    levels = np.array([10, -10, 5, -5, 0])
    if k % 512:
        return np.exp2(np.random.permutation(np.resize(levels, k // 32))).repeat(32)
    a = np.empty((k // 512, 16))
    for p in range(k // 512):
        a[p, :8] = np.random.permutation(np.resize(levels, 8))
        for g in range(8):
            far = levels[np.abs(levels - a[p, g]) >= 10]
            a[p, g + 8] = far[np.random.randint(len(far))]
    return np.exp2(a.ravel()).repeat(32)


def f64(x):
    return np.asarray(x).astype(np.float64)


def striped(idx):
    return np.tile(idx.reshape(-1, 16).T, (8, 1)).astype(np.uint16)


def unstriped(offs):
    return offs[:16].T.reshape(-1).astype(np.int64)


E2M1 = np.array([0.0, 0.5, 1.0, 1.5, 2.0, 3.0, 4.0, 6.0, -0.0, -0.5, -1.0, -1.5, -2.0, -3.0, -4.0, -6.0])


def pack_weight(w, fmt):
    k, n = w.shape
    w = f64(np.asarray(w, np.float32).astype(ml_dtypes.bfloat16)).reshape(k // 32, 32, n)
    amax = np.abs(w).max(1)
    if fmt == "e4m3":
        byte = np.frexp(amax)[1] - 1 + 127 - 7
    else:
        mant, ex = np.frexp(amax / 6.0)
        byte = np.where(mant > 0.5, ex, ex - 1) + 127
    byte = np.clip(np.where(amax > 0, byte, 1), 1, 254)
    scaled = (w * np.exp2(127.0 - byte)[:, None, :]).reshape(k, n).astype(np.float32)
    by_word = np.ascontiguousarray(scaled.reshape(k // 512, 128, 4, n).transpose(0, 1, 3, 2))
    if fmt == "e4m3":
        words = by_word.astype(ml_dtypes.float8_e4m3fn).view(np.uint8)
    else:
        c = by_word.astype(ml_dtypes.float4_e2m1fn).view(np.uint8) & 0xF
        words = (c[..., 0::2] | (c[..., 1::2] << 4)).reshape(k // 512, 128, 2 * n)
    return np.ascontiguousarray(words), np.ascontiguousarray(byte.astype(np.uint8).reshape(k // 512, 16, n))


def unpack_weight(words, scales, fmt):
    g, _, n = scales.shape
    words = np.ascontiguousarray(words).reshape(g, 128, n, -1)
    if fmt == "e4m3":
        vals = words.view(ml_dtypes.float8_e4m3fn).astype(np.float64)
    else:
        nib = np.empty((g, 128, n, 4), np.uint8)
        nib[..., 0::2] = words & 0xF
        nib[..., 1::2] = words >> 4
        vals = E2M1[nib]
    vals = vals * np.repeat(np.exp2(scales.astype(np.float64) - 127.0), 8, axis=1)[..., None]
    return vals.transpose(0, 1, 3, 2).reshape(g * 512, n)


def relu2(v):
    return np.maximum(v, 0.0) ** 2


K, T, E, C, H, N = 512, 512, 4, 256, 512, 128


def by_expert(wq, xq):
    return np.concatenate([wq[e].T @ xq[:, e * C:(e + 1) * C] for e in range(E)], axis=1)


def setup_inputs():
    n = np.random.standard_normal
    s = mx_kscale(K)
    u = mx_kscale(H)
    first = np.random.permutation(np.repeat(np.arange(E), T // E))
    second = (first + 1 + np.random.permutation(np.repeat(np.arange(E - 1), -(-T // (E - 1)))[:T])) % E
    while np.bincount(second, minlength=E).max() != T // E:
        load = np.bincount(second, minlength=E); hi, lo = int(load.argmax()), int(load.argmin())
        t = np.flatnonzero((second == hi) & (first != lo))[0]; second[t] = lo
    slot_token = np.empty(E * C, np.int64); pos = np.empty((2, T), np.int64); fill = np.zeros(E, np.int64)
    place = np.stack([np.random.permutation(C) for _ in range(E)])
    for r, deal in enumerate((first, second)):
        for t in np.random.permutation(T):
            e = deal[t]; j = e * C + place[e, fill[e]]; fill[e] += 1; slot_token[j] = t; pos[r, t] = j
    g = np.random.uniform(0.2, 0.8, T)
    partner = np.concatenate([np.random.permutation(T) for _ in range(-(-E * C // T))])[:E * C]
    x = pack_weight(n((K, T)) * s[:, None], "e4m3")
    w1 = [pack_weight(m, "e2m1") for m in n((E, K, H)) / np.sqrt(K) / s[None, :, None] * u]
    wp = [pack_weight(m, "e2m1") for m in n((E, K, H)) / np.sqrt(K) / s[None, :, None] * u]
    w2 = [pack_weight(m, "e2m1") for m in n((E, H, N)) / np.sqrt(H) / u[None, :, None] ** 2]
    return {
        "x_words": x[0],
        "x_scales": x[1],
        "w1_words": np.stack([m[0] for m in w1]),
        "w1_scales": np.stack([m[1] for m in w1]),
        "wp_words": np.stack([m[0] for m in wp]),
        "wp_scales": np.stack([m[1] for m in wp]),
        "w2_words": np.stack([m[0] for m in w2]),
        "w2_scales": np.stack([m[1] for m in w2]),
        "gate": np.stack([np.tile(g, (128, 1)), np.tile(1.0 - g, (128, 1))]).astype(np.float32),
        "offs": striped(slot_token),
        "pos1": striped(pos[0]),
        "pos2": striped(pos[1]),
        "offs2": striped(partner),
    }


def reference(x_words, x_scales, w1_words, w1_scales, wp_words, wp_scales, w2_words, w2_scales, gate, offs, pos1, pos2, offs2):
    w1 = np.stack([unpack_weight(w1_words[e], w1_scales[e], "e2m1") for e in range(E)])
    wp = np.stack([unpack_weight(wp_words[e], wp_scales[e], "e2m1") for e in range(E)])
    w2 = np.stack([unpack_weight(w2_words[e], w2_scales[e], "e2m1") for e in range(E)])
    idx, idx2 = unstriped(offs), unstriped(offs2)
    x = unpack_weight(x_words, x_scales, "e4m3")
    h = relu2(by_expert(w1, x[:, idx]) + by_expert(wp, x[:, idx2]))
    y = by_expert(w2, mxq(h, 0, "e4m3"))
    out = sum(f64(gate[r, :1]) * y[:, unstriped(p)] for r, p in enumerate((pos1, pos2)))
    return out

@@ -1,0 +1,203 @@
+from contextlib import ExitStack
+
+import concourse.mybir as mybir
+from concourse.masks import make_identity
+
+K, T, E, C, H, N = 512, 512, 4, 256, 512, 128
+S = E * C
+P = 128
+FLOPS = 2 * S * (2 * K * H + H * N)
+
+F32 = mybir.dt.float32
+BF16 = mybir.dt.bfloat16
+I32 = mybir.dt.int32
+U32 = mybir.dt.uint32
+U16 = mybir.dt.uint16
+U8 = mybir.dt.uint8
+FP8X4 = mybir.dt.float8_e4m3fn_x4
+FP4X4 = mybir.dt.float4_e2m1fn_x4
+ACT = mybir.ActivationFunctionType
+ALU = mybir.AluOpType
+
+
+def tile_moe_duo_relu2_kernel(
+    tc, x_words, x_scales, w1_words, w1_scales, wp_words, wp_scales, w2_words, w2_scales, gate, offs, pos1, pos2, offs2, out
+):
+    nc = tc.nc
+    with ExitStack() as ctx:
+        keep = ctx.enter_context(tc.tile_pool(name="keep", bufs=1))
+        ring = ctx.enter_context(tc.tile_pool(name="ring", bufs=3))
+        ps_keep = ctx.enter_context(tc.psum_pool(name="ps_keep", bufs=1))
+        ps_turn = ctx.enter_context(tc.psum_pool(name="ps_turn", bufs=3))
+
+        tok_list = keep.tile([P, S // 16], U16, name="tok_list")
+        par_list = keep.tile([P, S // 16], U16, name="par_list")
+        pos1_list = keep.tile([P, T // 16], U16, name="pos1_list")
+        pos2_list = keep.tile([P, T // 16], U16, name="pos2_list")
+        xw = keep.tile([P, T], I32, name="xw", align_bytes=64)
+        xs = keep.tile([P, T], U8, name="xs", align_bytes=64)
+        w1w = keep.tile([P, E, 2 * H], U8, name="w1w", align_bytes=64)
+        wpw = keep.tile([P, E, 2 * H], U8, name="wpw", align_bytes=64)
+        w2w = keep.tile([P, E, 2 * N], U8, name="w2w", align_bytes=64)
+        w1s = keep.tile([P, E * H], U8, name="w1s", align_bytes=64)
+        wps = keep.tile([P, E * H], U8, name="wps", align_bytes=64)
+        w2s = keep.tile([P, E * N], U8, name="w2s", align_bytes=64)
+        gates = keep.tile([P, 2, T], F32, name="gates", align_bytes=64)
+        ident = keep.tile([P, P], F32, name="ident", align_bytes=64)
+
+        for plane in (xs, w1s, wps, w2s):
+            nc.vector.memset(plane[:].bitcast(I32), 0)
+
+        def load_scales(queue, plane, src, rows):
+            by_row = src.rearrange("e s (q r) c -> r q (e s) c", r=4)
+            for r in rows:
+                dst = plane[r:P:32, :].bitcast(I32).rearrange("q (e c) -> q e c", e=src.shape[0])
+                queue.dma_start(dst, by_row[r].bitcast(I32))
+
+        def load_words(queue, tile, src, e0, e1):
+            queue.dma_start(tile[:, e0:e1, :].bitcast(I32), src[e0:e1, 0].rearrange("e p c -> p e c").bitcast(I32))
+
+        xs_rows = x_scales[0].rearrange("(q r) c -> r q c", r=4)
+
+        def load_x_scales(queue, rows):
+            for r in rows:
+                queue.dma_start(xs[r:P:32, :].bitcast(I32), xs_rows[r].bitcast(I32))
+
+        nc.sync.dma_start(tok_list[:], offs)
+        nc.scalar.dma_start(xw[:], x_words[0].rearrange("p t d -> p (t d)").bitcast(I32))
+        load_words(nc.gpsimd, wpw, wp_words, 0, 1)
+        load_x_scales(nc.sync, (0, 1))
+        load_x_scales(nc.scalar, (2, 3))
+        nc.sync.dma_start(par_list[:], offs2)
+        load_words(nc.sync, w1w, w1_words, 0, 1)
+        make_identity(nc, ident[:])
+        load_scales(nc.sync, w1s, w1_scales, range(4))
+        load_scales(nc.sync, wps, wp_scales, range(4))
+        load_words(nc.sync, w1w, w1_words, 1, 2)
+        load_words(nc.sync, wpw, wp_words, 1, 2)
+        load_words(nc.sync, w1w, w1_words, 2, 4)
+        load_words(nc.sync, wpw, wp_words, 2, 4)
+        load_words(nc.sync, w2w, w2_words, 0, 4)
+        load_scales(nc.sync, w2s, w2_scales, range(4))
+        nc.sync.dma_start(pos1_list[:], pos1)
+        nc.sync.dma_start(pos2_list[:], pos2)
+        nc.sync.dma_start(gates[:], gate.rearrange("r p t -> p r t"))
+
+        tok_w = keep.tile([P, 2 * P], U32, name="tok_w", align_bytes=64)
+        par_w = keep.tile([P, 3 * P], U32, name="par_w", align_bytes=64)
+        tok_s = keep.tile([P, 2 * P], U8, name="tok_s", align_bytes=64)
+        par_s = keep.tile([P, 3 * P], U8, name="par_s", align_bytes=64)
+
+        xw_u = xw[:].bitcast(U32)
+        sides = ((tok_w, tok_s, tok_list, 2, w1w, w1s), (par_w, par_s, par_list, 3, wpw, wps))
+
+        def gather(side, j):
+            gw, gs, lst, depth = sides[side][:4]
+            cols = slice(j % depth * P, (j % depth + 1) * P)
+            offsets = lst[:, j * P // 16 : (j + 1) * P // 16]
+            nc.vector.tensor_copy(gw[:, cols], xw_u.indirect(offsets))
+            nc.vector.tensor_copy(gs[:, cols], xs[:].indirect(offsets))
+
+        hb = keep.tile([P, S, 4], BF16, name="hb", align_bytes=64)
+        n_tiles = S // P
+        relu_of = {}
+        pre_banks = [ps_keep.tile([P, H], F32, name="pre%d" % i) for i in range(3)]
+        bank_of = [0, 1, 2, 0, 1, 2, 1, 2]
+
+        def first_layer(j):
+            e = j * P // C
+            pre = pre_banks[bank_of[j]]
+            for i, side in enumerate((0, 1) if j < 5 else (1, 0)):
+                gw, gs, lst, depth, ww, ws = sides[side]
+                cols = slice(j % depth * P, (j % depth + 1) * P)
+                nc.tensor.matmul_mx(
+                    pre[:],
+                    lhsT=gw[:, cols].bitcast(FP8X4),
+                    lhsT_scale=gs[:, cols],
+                    rhs=ww[:, e, :].bitcast(FP4X4),
+                    rhs_scale=ws[:, e * H : (e + 1) * H],
+                    start=(i == 0),
+                    stop=(i == 1),
+                )
+            pos_part = ring.tile([P, 4, P], F32, name="pos_part", align_bytes=64)
+            src = pre[:].rearrange("s (p t) -> s t p", t=4)
+            if j == n_tiles - 1:
+                nc.vector.tensor_scalar_max(pos_part[:], src, 0.0)
+            else:
+                nc.scalar.activation(pos_part[:], src, ACT.Relu)
+            relu_of[j] = pos_part
+
+        def turn_and_square(j):
+            turned = ps_turn.tile([P, 4, P], F32, name="turned")
+            for t in range(4):
+                nc.tensor.transpose(turned[:, t, :], relu_of[j][:, t, :], ident[:])
+            nc.scalar.activation(hb[:, j * P : (j + 1) * P, :], turned[:].rearrange("p t s -> p s t"), ACT.Square)
+
+        gather(0, 0)
+        gather(1, 0)
+        gather(0, 1)
+        gather(1, 1)
+        gather(1, 2)
+        for j in range(n_tiles):
+            first_layer(j)
+            if j + 2 < n_tiles:
+                gather(0, j + 2)
+            if j + 3 < n_tiles:
+                gather(1, j + 3)
+            if j > 0:
+                turn_and_square(j - 1)
+        turn_and_square(n_tiles - 1)
+
+        hw = keep.tile([P, S], U32, name="hw", align_bytes=64)
+        hs = keep.tile([P, S], U8, name="hs", align_bytes=64)
+        y = keep.tile([P, S], F32, name="y", align_bytes=64)
+
+        def quantize(a, b):
+            nc.vector.quantize_mx(hw[:, a:b].bitcast(FP8X4), hs[:, a:b], hb[:, a:b, :].rearrange("p s t -> p (s t)"))
+
+        def second_layer(bank, base, a, b):
+            e = a // C
+            nc.tensor.matmul_mx(
+                bank[:, a - base : b - base],
+                lhsT=w2w[:, e, :].bitcast(FP4X4),
+                lhsT_scale=w2s[:, e * N : (e + 1) * N],
+                rhs=hw[:, a:b].bitcast(FP8X4),
+                rhs_scale=hs[:, a:b],
+                start=True,
+                stop=True,
+            )
+
+        bank_mid = ps_keep.tile([P, H], F32, name="bank_mid")
+        bank_last = ps_keep.tile([P, H], F32, name="bank_last")
+        quantize(0, 256)
+        quantize(256, 512)
+        second_layer(pre_banks[1], 0, 0, 256)
+        second_layer(pre_banks[1], 0, 256, 512)
+        quantize(512, 768)
+        nc.vector.tensor_copy(y[:, 0:512], pre_banks[1][:])
+        second_layer(bank_mid, 512, 512, 768)
+        quantize(768, 896)
+        second_layer(bank_mid, 512, 768, 896)
+        quantize(896, 1024)
+        second_layer(bank_last, 896, 896, 1024)
+        nc.scalar.copy(y[:, 512:896], bank_mid[:, 0:384])
+        nc.scalar.copy(y[:, 896:1024], bank_last[:, 0:128])
+
+        part1 = keep.tile([P, T], F32, name="part1", align_bytes=64)
+        part2 = keep.tile([P, T], F32, name="part2", align_bytes=64)
+        res = keep.tile([P, T], F32, name="res", align_bytes=64)
+
+        def weigh(dst, lst, r, a, b):
+            nc.vector.tensor_tensor(dst[:, a:b], y[:].indirect(lst[:, a // 16 : b // 16]), gates[:, r, a:b], ALU.mult)
+
+        def finish(a, b):
+            nc.vector.tensor_tensor(res[:, a:b], part1[:, a:b], part2[:, a:b], ALU.add)
+            nc.sync.dma_start(out[:, a:b], res[:, a:b])
+
+        half = T // 2
+        weigh(part1, pos1_list, 0, 0, half)
+        weigh(part2, pos2_list, 1, 0, half)
+        weigh(part1, pos1_list, 0, half, T)
+        finish(0, half)
+        weigh(part2, pos2_list, 1, half, T)
+        finish(half, T)

@@ -83,18 +83,20 @@ def tile_moe_duo_relu2_kernel(
         nc.sync.dma_start(pos2_list[:], pos2)
         nc.sync.dma_start(gates[:], gate.rearrange("r p t -> p r t"))
 
-        tok_w = keep.tile([P, 2 * P], U32, name="tok_w", align_bytes=64)
-        par_w = keep.tile([P, 3 * P], U32, name="par_w", align_bytes=64)
-        tok_s = keep.tile([P, 2 * P], U8, name="tok_s", align_bytes=64)
-        par_s = keep.tile([P, 3 * P], U8, name="par_s", align_bytes=64)
+        tok_w = keep.tile([P, 4 * P], U32, name="tok_w", align_bytes=64)
+        par_w = keep.tile([P, 4 * P], U32, name="par_w", align_bytes=64)
+        tok_s = keep.tile([P, 4 * P], U8, name="tok_s", align_bytes=64)
+        par_s = keep.tile([P, 4 * P], U8, name="par_s", align_bytes=64)
 
         xw_u = xw[:].bitcast(U32)
-        sides = ((tok_w, tok_s, tok_list, 2, w1w, w1s), (par_w, par_s, par_list, 3, wpw, wps))
+        tok_place = [1, 2, 0, 1, 2, 3, 0, 1]
+        par_place = [0, 2, 3, 0, 1, 2, 3, 0]
+        sides = ((tok_w, tok_s, tok_list, tok_place, w1w, w1s), (par_w, par_s, par_list, par_place, wpw, wps))
 
-        def gather(side, j):
-            gw, gs, lst, depth = sides[side][:4]
-            cols = slice(j % depth * P, (j % depth + 1) * P)
-            offsets = lst[:, j * P // 16 : (j + 1) * P // 16]
+        def gather(side, j, count):
+            gw, gs, lst, place = sides[side][:4]
+            cols = slice(place[j] * P, (place[j] + count) * P)
+            offsets = lst[:, j * P // 16 : (j + count) * P // 16]
             nc.vector.tensor_copy(gw[:, cols], xw_u.indirect(offsets))
             nc.vector.tensor_copy(gs[:, cols], xs[:].indirect(offsets))
 
@@ -107,9 +109,9 @@ def tile_moe_duo_relu2_kernel(
         def first_layer(j):
             e = j * P // C
             pre = pre_banks[bank_of[j]]
-            for i, side in enumerate((0, 1) if j < 5 else (1, 0)):
-                gw, gs, lst, depth, ww, ws = sides[side]
-                cols = slice(j % depth * P, (j % depth + 1) * P)
+            for i, side in enumerate((0, 1) if j in (0, 3, 5, 7) else (1, 0)):
+                gw, gs, lst, place, ww, ws = sides[side]
+                cols = slice(place[j] * P, (place[j] + 1) * P)
                 nc.tensor.matmul_mx(
                     pre[:],
                     lhsT=gw[:, cols].bitcast(FP8X4),
@@ -133,17 +135,14 @@ def tile_moe_duo_relu2_kernel(
                 nc.tensor.transpose(turned[:, t, :], relu_of[j][:, t, :], ident[:])
             nc.scalar.activation(hb[:, j * P : (j + 1) * P, :], turned[:].rearrange("p t s -> p s t"), ACT.Square)
 
-        gather(0, 0)
-        gather(1, 0)
-        gather(0, 1)
-        gather(1, 1)
-        gather(1, 2)
+        after = {0: ((0, 2, 2), (1, 3, 2)), 1: ((0, 4, 2),), 2: ((1, 5, 2), (0, 6, 1)), 3: ((0, 7, 1), (1, 7, 1))}
+        gather(0, 0, 2)
+        gather(1, 0, 1)
+        gather(1, 1, 2)
         for j in range(n_tiles):
             first_layer(j)
-            if j + 2 < n_tiles:
-                gather(0, j + 2)
-            if j + 3 < n_tiles:
-                gather(1, j + 3)
+            for piece in after.get(j, ()):
+                gather(*piece)
             if j > 0:
                 turn_and_square(j - 1)
         turn_and_square(n_tiles - 1)

@@ -48,6 +48,11 @@ def tile_moe_duo_relu2_kernel(
         for plane in (xs, w1s, wps, w2s):
             nc.vector.memset(plane[:].bitcast(I32), 0)
 
+        hw = keep.tile([P, S], U32, name="hw", align_bytes=64)
+        hs = keep.tile([P, S], U8, name="hs", align_bytes=64)
+        nc.vector.memset(hw[:, 0:P].bitcast(I32), 0)
+        nc.vector.memset(hs[:, 0:P].bitcast(I32), 0)
+
         def load_scales(queue, plane, src, rows):
             by_row = src.rearrange("e s (q r) c -> r q (e s) c", r=4)
             for r in rows:
@@ -71,6 +76,17 @@ def tile_moe_duo_relu2_kernel(
         nc.sync.dma_start(par_list[:], offs2)
         load_words(nc.sync, w1w, w1_words, 0, 1)
         make_identity(nc, ident[:])
+        pre_banks = [ps_keep.tile([P, H], F32, name="pre%d" % i) for i in range(3)]
+        for i in range(4):
+            nc.tensor.matmul_mx(
+                pre_banks[i % 3][:],
+                lhsT=hw[:, 0:P].bitcast(FP8X4),
+                lhsT_scale=hs[:, 0:P],
+                rhs=w1w[:, 0, :].bitcast(FP4X4),
+                rhs_scale=w2s[:],
+                start=True,
+                stop=True,
+            )
         load_scales(nc.sync, w1s, w1_scales, range(4))
         load_scales(nc.sync, wps, wp_scales, range(4))
         load_words(nc.sync, w1w, w1_words, 1, 2)
@@ -103,7 +119,6 @@ def tile_moe_duo_relu2_kernel(
         hb = keep.tile([P, S, 4], BF16, name="hb", align_bytes=64)
         n_tiles = S // P
         relu_of = {}
-        pre_banks = [ps_keep.tile([P, H], F32, name="pre%d" % i) for i in range(3)]
         bank_of = [0, 1, 2, 0, 1, 2, 1, 2]
 
         def first_layer(j):
@@ -147,8 +162,6 @@ def tile_moe_duo_relu2_kernel(
                 turn_and_square(j - 1)
         turn_and_square(n_tiles - 1)
 
-        hw = keep.tile([P, S], U32, name="hw", align_bytes=64)
-        hs = keep.tile([P, S], U8, name="hs", align_bytes=64)
         y = keep.tile([P, S], F32, name="y", align_bytes=64)
 
         def quantize(a, b):
@@ -194,9 +207,8 @@ def tile_moe_duo_relu2_kernel(
             nc.sync.dma_start(out[:, a:b], res[:, a:b])
 
         half = T // 2
-        weigh(part1, pos1_list, 0, 0, half)
+        weigh(part1, pos1_list, 0, 0, T)
         weigh(part2, pos2_list, 1, 0, half)
-        weigh(part1, pos1_list, 0, half, T)
-        finish(0, half)
         weigh(part2, pos2_list, 1, half, T)
+        finish(0, half)
         finish(half, T)

@@ -50,8 +50,6 @@ def tile_moe_duo_relu2_kernel(
 
         hw = keep.tile([P, S], U32, name="hw", align_bytes=64)
         hs = keep.tile([P, S], U8, name="hs", align_bytes=64)
-        nc.vector.memset(hw[:, 0:P].bitcast(I32), 0)
-        nc.vector.memset(hs[:, 0:P].bitcast(I32), 0)
 
         def load_scales(queue, plane, src, rows):
             by_row = src.rearrange("e s (q r) c -> r q (e s) c", r=4)
@@ -77,16 +75,6 @@ def tile_moe_duo_relu2_kernel(
         load_words(nc.sync, w1w, w1_words, 0, 1)
         make_identity(nc, ident[:])
         pre_banks = [ps_keep.tile([P, H], F32, name="pre%d" % i) for i in range(3)]
-        for i in range(4):
-            nc.tensor.matmul_mx(
-                pre_banks[i % 3][:],
-                lhsT=hw[:, 0:P].bitcast(FP8X4),
-                lhsT_scale=hs[:, 0:P],
-                rhs=w1w[:, 0, :].bitcast(FP4X4),
-                rhs_scale=w2s[:],
-                start=True,
-                stop=True,
-            )
         load_scales(nc.sync, w1s, w1_scales, range(4))
         load_scales(nc.sync, wps, wp_scales, range(4))
         load_words(nc.sync, w1w, w1_words, 1, 2)
@@ -106,15 +94,18 @@ def tile_moe_duo_relu2_kernel(
 
         xw_u = xw[:].bitcast(U32)
         tok_place = [1, 2, 0, 1, 2, 3, 0, 1]
-        par_place = [0, 2, 3, 0, 1, 2, 3, 0]
+        par_place = [1, 2, 3, 0, 1, 2, 3, 0]
         sides = ((tok_w, tok_s, tok_list, tok_place, w1w, w1s), (par_w, par_s, par_list, par_place, wpw, wps))
 
-        def gather(side, j, count):
-            gw, gs, lst, place = sides[side][:4]
+        def gather_sort(sort, side, j, count):
+            place = sides[side][3]
             cols = slice(place[j] * P, (place[j] + count) * P)
-            offsets = lst[:, j * P // 16 : (j + count) * P // 16]
-            nc.vector.tensor_copy(gw[:, cols], xw_u.indirect(offsets))
-            nc.vector.tensor_copy(gs[:, cols], xs[:].indirect(offsets))
+            offsets = sides[side][2][:, j * P // 16 : (j + count) * P // 16]
+            nc.vector.tensor_copy(sides[side][sort][:, cols], (xw_u, xs[:])[sort].indirect(offsets))
+
+        def gather(side, j, count):
+            gather_sort(0, side, j, count)
+            gather_sort(1, side, j, count)
 
         hb = keep.tile([P, S, 4], BF16, name="hb", align_bytes=64)
         n_tiles = S // P
@@ -139,7 +130,8 @@ def tile_moe_duo_relu2_kernel(
             pos_part = ring.tile([P, 4, P], F32, name="pos_part", align_bytes=64)
             src = pre[:].rearrange("s (p t) -> s t p", t=4)
             if j == n_tiles - 1:
-                nc.vector.tensor_scalar_max(pos_part[:], src, 0.0)
+                for t in (0, 2):
+                    nc.vector.tensor_scalar_max(pos_part[:, t : t + 2, :], src[:, t : t + 2, :], 0.0)
             else:
                 nc.scalar.activation(pos_part[:], src, ACT.Relu)
             relu_of[j] = pos_part
@@ -150,10 +142,11 @@ def tile_moe_duo_relu2_kernel(
                 nc.tensor.transpose(turned[:, t, :], relu_of[j][:, t, :], ident[:])
             nc.scalar.activation(hb[:, j * P : (j + 1) * P, :], turned[:].rearrange("p t s -> p s t"), ACT.Square)
 
-        after = {0: ((0, 2, 2), (1, 3, 2)), 1: ((0, 4, 2),), 2: ((1, 5, 2), (0, 6, 1)), 3: ((0, 7, 1), (1, 7, 1))}
+        after = {0: ((0, 2, 2), (1, 3, 2)), 1: ((0, 4, 2),), 2: ((1, 5, 2),), 3: ((0, 6, 2), (1, 7, 1))}
         gather(0, 0, 2)
-        gather(1, 0, 1)
-        gather(1, 1, 2)
+        gather_sort(0, 1, 0, 3)
+        gather_sort(1, 1, 0, 1)
+        gather_sort(1, 1, 1, 2)
         for j in range(n_tiles):
             first_layer(j)
             for piece in after.get(j, ()):

@@ -8,6 +8,13 @@ S = E * C
 P = 128
 FLOPS = 2 * S * (2 * K * H + H * N)
 
+GROUPS = S // P
+PACK = 4
+LIST_ROWS = 16
+PLACES = 4
+TOKENS, PARTNERS = 0, 1
+WORDS, SCALES = 0, 1
+
 F32 = mybir.dt.float32
 BF16 = mybir.dt.bfloat16
 I32 = mybir.dt.int32
@@ -30,37 +37,40 @@ def tile_moe_duo_relu2_kernel(
         ps_keep = ctx.enter_context(tc.psum_pool(name="ps_keep", bufs=1))
         ps_turn = ctx.enter_context(tc.psum_pool(name="ps_turn", bufs=3))
 
-        tok_list = keep.tile([P, S // 16], U16, name="tok_list")
-        par_list = keep.tile([P, S // 16], U16, name="par_list")
-        pos1_list = keep.tile([P, T // 16], U16, name="pos1_list")
-        pos2_list = keep.tile([P, T // 16], U16, name="pos2_list")
+        tok_list = keep.tile([P, S // LIST_ROWS], U16, name="tok_list")
+        par_list = keep.tile([P, S // LIST_ROWS], U16, name="par_list")
+        pos1_list = keep.tile([P, T // LIST_ROWS], U16, name="pos1_list")
+        pos2_list = keep.tile([P, T // LIST_ROWS], U16, name="pos2_list")
         xw = keep.tile([P, T], I32, name="xw", align_bytes=64)
         xs = keep.tile([P, T], U8, name="xs", align_bytes=64)
         w1w = keep.tile([P, E, 2 * H], U8, name="w1w", align_bytes=64)
         wpw = keep.tile([P, E, 2 * H], U8, name="wpw", align_bytes=64)
         w2w = keep.tile([P, E, 2 * N], U8, name="w2w", align_bytes=64)
-        w1s = keep.tile([P, E * H], U8, name="w1s", align_bytes=64)
-        wps = keep.tile([P, E * H], U8, name="wps", align_bytes=64)
-        w2s = keep.tile([P, E * N], U8, name="w2s", align_bytes=64)
+        w1s_pad = keep.tile([P, E * H + 4], U8, name="w1s_pad", align_bytes=64)
+        wps_pad = keep.tile([P, E * H + 4], U8, name="wps_pad", align_bytes=64)
+        w2s_pad = keep.tile([P, E * N + 4], U8, name="w2s_pad", align_bytes=64)
         gates = keep.tile([P, 2, T], F32, name="gates", align_bytes=64)
         ident = keep.tile([P, P], F32, name="ident", align_bytes=64)
 
-        for plane in (xs, w1s, wps, w2s):
-            nc.vector.memset(plane[:].bitcast(I32), 0)
+        w1s = w1s_pad[:, 0 : E * H]
+        wps = wps_pad[:, 0 : E * H]
+        w2s = w2s_pad[:, 0 : E * N]
+        for scale_tile in (xs, w1s_pad, wps_pad, w2s_pad):
+            nc.vector.memset(scale_tile[:].bitcast(I32), 0)
 
         hw = keep.tile([P, S], U32, name="hw", align_bytes=64)
         hs = keep.tile([P, S], U8, name="hs", align_bytes=64)
 
-        def load_scales(queue, plane, src, rows):
-            by_row = src.rearrange("e s (q r) c -> r q (e s) c", r=4)
-            for r in rows:
-                dst = plane[r:P:32, :].bitcast(I32).rearrange("q (e c) -> q e c", e=src.shape[0])
-                queue.dma_start(dst, by_row[r].bitcast(I32))
+        def load_scales(scale_tile, src):
+            by_row = src.rearrange("e s (q r) c -> r q (e s) c", r=PACK)
+            for r in range(PACK):
+                dst = scale_tile[r:P:32, :].bitcast(I32).rearrange("q (e c) -> q e c", e=E)
+                nc.sync.dma_start(dst, by_row[r].bitcast(I32))
 
         def load_words(queue, tile, src, e0, e1):
             queue.dma_start(tile[:, e0:e1, :].bitcast(I32), src[e0:e1, 0].rearrange("e p c -> p e c").bitcast(I32))
 
-        xs_rows = x_scales[0].rearrange("(q r) c -> r q c", r=4)
+        xs_rows = x_scales[0].rearrange("(q r) c -> r q c", r=PACK)
 
         def load_x_scales(queue, rows):
             for r in rows:
@@ -75,61 +85,72 @@ def tile_moe_duo_relu2_kernel(
         load_words(nc.sync, w1w, w1_words, 0, 1)
         make_identity(nc, ident[:])
         pre_banks = [ps_keep.tile([P, H], F32, name="pre%d" % i) for i in range(3)]
-        load_scales(nc.sync, w1s, w1_scales, range(4))
-        load_scales(nc.sync, wps, wp_scales, range(4))
-        load_words(nc.sync, w1w, w1_words, 1, 2)
-        load_words(nc.sync, wpw, wp_words, 1, 2)
-        load_words(nc.sync, w1w, w1_words, 2, 4)
-        load_words(nc.sync, wpw, wp_words, 2, 4)
-        load_words(nc.sync, w2w, w2_words, 0, 4)
-        load_scales(nc.sync, w2s, w2_scales, range(4))
+        load_scales(w1s, w1_scales)
+        load_scales(wps, wp_scales)
+        for e0, e1 in ((1, 2), (2, E)):
+            load_words(nc.sync, w1w, w1_words, e0, e1)
+            load_words(nc.sync, wpw, wp_words, e0, e1)
+        load_words(nc.sync, w2w, w2_words, 0, E)
+        load_scales(w2s, w2_scales)
         nc.sync.dma_start(pos1_list[:], pos1)
         nc.sync.dma_start(pos2_list[:], pos2)
         nc.sync.dma_start(gates[:], gate.rearrange("r p t -> p r t"))
 
-        tok_w = keep.tile([P, 4 * P], U32, name="tok_w", align_bytes=64)
-        par_w = keep.tile([P, 4 * P], U32, name="par_w", align_bytes=64)
-        tok_s = keep.tile([P, 4 * P], U8, name="tok_s", align_bytes=64)
-        par_s = keep.tile([P, 4 * P], U8, name="par_s", align_bytes=64)
+        tok_w = keep.tile([P, PLACES * P], U32, name="tok_w", align_bytes=64)
+        par_w = keep.tile([P, PLACES * P], U32, name="par_w", align_bytes=64)
+        tok_s = keep.tile([P, PLACES * P], U8, name="tok_s", align_bytes=64)
+        par_s = keep.tile([P, PLACES * P], U8, name="par_s", align_bytes=64)
 
-        xw_u = xw[:].bitcast(U32)
-        tok_place = [1, 2, 0, 1, 2, 3, 0, 1]
-        par_place = [1, 2, 3, 0, 1, 2, 3, 0]
-        sides = ((tok_w, tok_s, tok_list, tok_place, w1w, w1s), (par_w, par_s, par_list, par_place, wpw, wps))
+        windows = (xw[:].bitcast(U32), xs[:])
+        gathered = ((tok_w, tok_s), (par_w, par_s))
+        lists = (tok_list, par_list)
+        weights = ((w1w, w1s), (wpw, wps))
+
+        first_count = (2, 3)
+
+        def place(side, j):
+            return j + 1 if j < first_count[side] else (j - first_count[side]) % PLACES
 
         def gather_sort(sort, side, j, count):
-            place = sides[side][3]
-            cols = slice(place[j] * P, (place[j] + count) * P)
-            offsets = sides[side][2][:, j * P // 16 : (j + count) * P // 16]
-            nc.vector.tensor_copy(sides[side][sort][:, cols], (xw_u, xs[:])[sort].indirect(offsets))
+            cols = slice(place(side, j) * P, (place(side, j) + count) * P)
+            offsets = lists[side][:, j * P // LIST_ROWS : (j + count) * P // LIST_ROWS]
+            nc.vector.tensor_copy(gathered[side][sort][:, cols], windows[sort].indirect(offsets))
 
         def gather(side, j, count):
-            gather_sort(0, side, j, count)
-            gather_sort(1, side, j, count)
+            gather_sort(WORDS, side, j, count)
+            gather_sort(SCALES, side, j, count)
 
-        hb = keep.tile([P, S, 4], BF16, name="hb", align_bytes=64)
-        n_tiles = S // P
+        gathers_behind = {}
+        for j in range(first_count[TOKENS], GROUPS):
+            side, count = j % 2, min(2, GROUPS - j)
+            taken = range(place(side, j), place(side, j) + count)
+            holder = max(old for old in range(j) if place(side, old) in taken)
+            gathers_behind.setdefault(holder, []).append((side, j, count))
+
+        hb = keep.tile([P, S, PACK], BF16, name="hb", align_bytes=64)
         relu_of = {}
-        bank_of = [0, 1, 2, 0, 1, 2, 1, 2]
+
+        def bank_of(j):
+            return pre_banks[j % 3] if j < GROUPS - 2 else bank_of(j - 2)
 
         def first_layer(j):
             e = j * P // C
-            pre = pre_banks[bank_of[j]]
-            for i, side in enumerate((0, 1) if j in (0, 3, 5, 7) else (1, 0)):
-                gw, gs, lst, place, ww, ws = sides[side]
-                cols = slice(place[j] * P, (place[j] + 1) * P)
+            pre = bank_of(j)
+            opener = TOKENS if j == 0 or (j > 1 and j % 2 == 1) else PARTNERS
+            for side in (opener, 1 - opener):
+                cols = slice(place(side, j) * P, (place(side, j) + 1) * P)
                 nc.tensor.matmul_mx(
                     pre[:],
-                    lhsT=gw[:, cols].bitcast(FP8X4),
-                    lhsT_scale=gs[:, cols],
-                    rhs=ww[:, e, :].bitcast(FP4X4),
-                    rhs_scale=ws[:, e * H : (e + 1) * H],
-                    start=(i == 0),
-                    stop=(i == 1),
+                    lhsT=gathered[side][WORDS][:, cols].bitcast(FP8X4),
+                    lhsT_scale=gathered[side][SCALES][:, cols],
+                    rhs=weights[side][WORDS][:, e, :].bitcast(FP4X4),
+                    rhs_scale=weights[side][SCALES][:, e * H : (e + 1) * H],
+                    start=(side == opener),
+                    stop=(side != opener),
                 )
-            pos_part = ring.tile([P, 4, P], F32, name="pos_part", align_bytes=64)
-            src = pre[:].rearrange("s (p t) -> s t p", t=4)
-            if j == n_tiles - 1:
+            pos_part = ring.tile([P, PACK, P], F32, name="pos_part", align_bytes=64)
+            src = pre[:].rearrange("s (p t) -> s t p", t=PACK)
+            if j == GROUPS - 1:
                 for t in (0, 2):
                     nc.vector.tensor_scalar_max(pos_part[:, t : t + 2, :], src[:, t : t + 2, :], 0.0)
             else:
@@ -137,23 +158,22 @@ def tile_moe_duo_relu2_kernel(
             relu_of[j] = pos_part
 
         def turn_and_square(j):
-            turned = ps_turn.tile([P, 4, P], F32, name="turned")
-            for t in range(4):
+            turned = ps_turn.tile([P, PACK, P], F32, name="turned")
+            for t in range(PACK):
                 nc.tensor.transpose(turned[:, t, :], relu_of[j][:, t, :], ident[:])
             nc.scalar.activation(hb[:, j * P : (j + 1) * P, :], turned[:].rearrange("p t s -> p s t"), ACT.Square)
 
-        after = {0: ((0, 2, 2), (1, 3, 2)), 1: ((0, 4, 2),), 2: ((1, 5, 2),), 3: ((0, 6, 2), (1, 7, 1))}
-        gather(0, 0, 2)
-        gather_sort(0, 1, 0, 3)
-        gather_sort(1, 1, 0, 1)
-        gather_sort(1, 1, 1, 2)
-        for j in range(n_tiles):
+        gather(TOKENS, 0, first_count[TOKENS])
+        gather_sort(WORDS, PARTNERS, 0, first_count[PARTNERS])
+        gather_sort(SCALES, PARTNERS, 0, 1)
+        gather_sort(SCALES, PARTNERS, 1, first_count[PARTNERS] - 1)
+        for j in range(GROUPS):
             first_layer(j)
-            for piece in after.get(j, ()):
+            for piece in gathers_behind.get(j, ()):
                 gather(*piece)
             if j > 0:
                 turn_and_square(j - 1)
-        turn_and_square(n_tiles - 1)
+        turn_and_square(GROUPS - 1)
 
         y = keep.tile([P, S], F32, name="y", align_bytes=64)
 
@@ -172,28 +192,31 @@ def tile_moe_duo_relu2_kernel(
                 stop=True,
             )
 
+        bank_first = bank_of(GROUPS - 2)
         bank_mid = ps_keep.tile([P, H], F32, name="bank_mid")
         bank_last = ps_keep.tile([P, H], F32, name="bank_last")
-        quantize(0, 256)
-        quantize(256, 512)
-        second_layer(pre_banks[1], 0, 0, 256)
-        second_layer(pre_banks[1], 0, 256, 512)
-        quantize(512, 768)
-        nc.vector.tensor_copy(y[:, 0:512], pre_banks[1][:])
-        second_layer(bank_mid, 512, 512, 768)
-        quantize(768, 896)
-        second_layer(bank_mid, 512, 768, 896)
-        quantize(896, 1024)
-        second_layer(bank_last, 896, 896, 1024)
-        nc.scalar.copy(y[:, 512:896], bank_mid[:, 0:384])
-        nc.scalar.copy(y[:, 896:1024], bank_last[:, 0:128])
+        mid, last = 2 * C, S - P
+        quantize(0, C)
+        quantize(C, mid)
+        second_layer(bank_first, 0, 0, C)
+        second_layer(bank_first, 0, C, mid)
+        quantize(mid, mid + C)
+        nc.vector.tensor_copy(y[:, 0:mid], bank_first[:])
+        second_layer(bank_mid, mid, mid, mid + C)
+        quantize(mid + C, last)
+        second_layer(bank_mid, mid, mid + C, last)
+        quantize(last, S)
+        second_layer(bank_last, last, last, S)
+        nc.scalar.copy(y[:, mid:last], bank_mid[:, 0 : last - mid])
+        nc.scalar.copy(y[:, last:S], bank_last[:, 0:P])
 
         part1 = keep.tile([P, T], F32, name="part1", align_bytes=64)
         part2 = keep.tile([P, T], F32, name="part2", align_bytes=64)
         res = keep.tile([P, T], F32, name="res", align_bytes=64)
 
         def weigh(dst, lst, r, a, b):
-            nc.vector.tensor_tensor(dst[:, a:b], y[:].indirect(lst[:, a // 16 : b // 16]), gates[:, r, a:b], ALU.mult)
+            offsets = lst[:, a // LIST_ROWS : b // LIST_ROWS]
+            nc.vector.tensor_tensor(dst[:, a:b], y[:].indirect(offsets), gates[:, r, a:b], ALU.mult)
 
         def finish(a, b):
             nc.vector.tensor_tensor(res[:, a:b], part1[:, a:b], part2[:, a:b], ALU.add)

@@ -11,7 +11,6 @@ FLOPS = 2 * S * (2 * K * H + H * N)
 GROUPS = S // P
 PACK = 4
 LIST_ROWS = 16
-PLACES = 4
 TOKENS, PARTNERS = 0, 1
 WORDS, SCALES = 0, 1
 
@@ -33,7 +32,7 @@ def tile_moe_duo_relu2_kernel(
     nc = tc.nc
     with ExitStack() as ctx:
         keep = ctx.enter_context(tc.tile_pool(name="keep", bufs=1))
-        ring = ctx.enter_context(tc.tile_pool(name="ring", bufs=3))
+        ring = ctx.enter_context(tc.tile_pool(name="ring", bufs=4))
         ps_keep = ctx.enter_context(tc.psum_pool(name="ps_keep", bufs=1))
         ps_turn = ctx.enter_context(tc.psum_pool(name="ps_turn", bufs=3))
 
@@ -41,7 +40,7 @@ def tile_moe_duo_relu2_kernel(
         par_list = keep.tile([P, S // LIST_ROWS], U16, name="par_list")
         pos1_list = keep.tile([P, T // LIST_ROWS], U16, name="pos1_list")
         pos2_list = keep.tile([P, T // LIST_ROWS], U16, name="pos2_list")
-        xw = keep.tile([P, T], I32, name="xw", align_bytes=64)
+        xw = keep.tile([P, T], I32, name="xw", tag="xw", align_bytes=64)
         xs = keep.tile([P, T], U8, name="xs", align_bytes=64)
         w1w = keep.tile([P, E, 2 * H], U8, name="w1w", align_bytes=64)
         wpw = keep.tile([P, E, 2 * H], U8, name="wpw", align_bytes=64)
@@ -58,14 +57,11 @@ def tile_moe_duo_relu2_kernel(
         for scale_tile in (xs, w1s_pad, wps_pad, w2s_pad):
             nc.vector.memset(scale_tile[:].bitcast(I32), 0)
 
-        hw = keep.tile([P, S], U32, name="hw", align_bytes=64)
-        hs = keep.tile([P, S], U8, name="hs", align_bytes=64)
-
-        def load_scales(scale_tile, src):
+        def load_scales(queue, scale_tile, src):
             by_row = src.rearrange("e s (q r) c -> r q (e s) c", r=PACK)
             for r in range(PACK):
                 dst = scale_tile[r:P:32, :].bitcast(I32).rearrange("q (e c) -> q e c", e=E)
-                nc.sync.dma_start(dst, by_row[r].bitcast(I32))
+                queue.dma_start(dst, by_row[r].bitcast(I32))
 
         def load_words(queue, tile, src, e0, e1):
             queue.dma_start(tile[:, e0:e1, :].bitcast(I32), src[e0:e1, 0].rearrange("e p c -> p e c").bitcast(I32))
@@ -79,83 +75,78 @@ def tile_moe_duo_relu2_kernel(
         nc.sync.dma_start(tok_list[:], offs)
         nc.scalar.dma_start(xw[:], x_words[0].rearrange("p t d -> p (t d)").bitcast(I32))
         load_words(nc.gpsimd, wpw, wp_words, 0, 1)
-        load_x_scales(nc.sync, (0, 1))
-        load_x_scales(nc.scalar, (2, 3))
         nc.sync.dma_start(par_list[:], offs2)
-        load_words(nc.sync, w1w, w1_words, 0, 1)
+        load_x_scales(nc.scalar, (2, 3))
+        load_x_scales(nc.sync, (0, 1))
+        load_words(nc.scalar, w1w, w1_words, 0, 1)
         make_identity(nc, ident[:])
         pre_banks = [ps_keep.tile([P, H], F32, name="pre%d" % i) for i in range(3)]
-        load_scales(w1s, w1_scales)
-        load_scales(wps, wp_scales)
+        load_scales(nc.sync, w1s, w1_scales)
+        load_scales(nc.scalar, wps, wp_scales)
         for e0, e1 in ((1, 2), (2, E)):
             load_words(nc.sync, w1w, w1_words, e0, e1)
             load_words(nc.sync, wpw, wp_words, e0, e1)
         load_words(nc.sync, w2w, w2_words, 0, E)
-        load_scales(w2s, w2_scales)
+        load_scales(nc.sync, w2s, w2_scales)
         nc.sync.dma_start(pos1_list[:], pos1)
         nc.sync.dma_start(pos2_list[:], pos2)
         nc.sync.dma_start(gates[:], gate.rearrange("r p t -> p r t"))
 
-        tok_w = keep.tile([P, PLACES * P], U32, name="tok_w", align_bytes=64)
-        par_w = keep.tile([P, PLACES * P], U32, name="par_w", align_bytes=64)
-        tok_s = keep.tile([P, PLACES * P], U8, name="tok_s", align_bytes=64)
-        par_s = keep.tile([P, PLACES * P], U8, name="par_s", align_bytes=64)
+        tok_w = keep.tile([P, 4 * P], U32, name="tok_w", align_bytes=64)
+        par_w = keep.tile([P, 4 * P], U32, name="par_w", align_bytes=64)
+        tok_s = keep.tile([P, 5 * P], U8, name="tok_s", align_bytes=64)
+        par_s = keep.tile([P, 5 * P], U8, name="par_s", align_bytes=64)
 
         windows = (xw[:].bitcast(U32), xs[:])
         gathered = ((tok_w, tok_s), (par_w, par_s))
         lists = (tok_list, par_list)
         weights = ((w1w, w1s), (wpw, wps))
 
-        first_count = (2, 3)
+        places = ((1, 2, 3, 0, 1, 2, 3, 2), (0, 1, 2, 3, 4, 0, 1, 3))
 
-        def place(side, j):
-            return j + 1 if j < first_count[side] else (j - first_count[side]) % PLACES
-
-        def gather_sort(sort, side, j, count):
-            cols = slice(place(side, j) * P, (place(side, j) + count) * P)
+        def gather_side(sort, side, j, count):
+            cols = slice(places[sort][j] * P, (places[sort][j] + count) * P)
             offsets = lists[side][:, j * P // LIST_ROWS : (j + count) * P // LIST_ROWS]
             nc.vector.tensor_copy(gathered[side][sort][:, cols], windows[sort].indirect(offsets))
 
-        def gather(side, j, count):
-            gather_sort(WORDS, side, j, count)
-            gather_sort(SCALES, side, j, count)
-
-        gathers_behind = {}
-        for j in range(first_count[TOKENS], GROUPS):
-            side, count = j % 2, min(2, GROUPS - j)
-            taken = range(place(side, j), place(side, j) + count)
-            holder = max(old for old in range(j) if place(side, old) in taken)
-            gathers_behind.setdefault(holder, []).append((side, j, count))
+        def gather(sort, j, count):
+            gather_side(sort, TOKENS, j, count)
+            gather_side(sort, PARTNERS, j, count)
 
         hb = keep.tile([P, S, PACK], BF16, name="hb", align_bytes=64)
         relu_of = {}
+        bank_of = [pre_banks[i] for i in (0, 1, 2, 1, 0, 1, 2, 1)]
 
-        def bank_of(j):
-            return pre_banks[j % 3] if j < GROUPS - 2 else bank_of(j - 2)
-
-        def first_layer(j):
+        def sums(j):
             e = j * P // C
-            pre = bank_of(j)
-            opener = TOKENS if j == 0 or (j > 1 and j % 2 == 1) else PARTNERS
-            for side in (opener, 1 - opener):
-                cols = slice(place(side, j) * P, (place(side, j) + 1) * P)
+            for side in (TOKENS, PARTNERS):
+                wcols = slice(places[WORDS][j] * P, (places[WORDS][j] + 1) * P)
+                scols = slice(places[SCALES][j] * P, (places[SCALES][j] + 1) * P)
                 nc.tensor.matmul_mx(
-                    pre[:],
-                    lhsT=gathered[side][WORDS][:, cols].bitcast(FP8X4),
-                    lhsT_scale=gathered[side][SCALES][:, cols],
+                    bank_of[j][:],
+                    lhsT=gathered[side][WORDS][:, wcols].bitcast(FP8X4),
+                    lhsT_scale=gathered[side][SCALES][:, scols],
                     rhs=weights[side][WORDS][:, e, :].bitcast(FP4X4),
                     rhs_scale=weights[side][SCALES][:, e * H : (e + 1) * H],
-                    start=(side == opener),
-                    stop=(side != opener),
+                    start=(side == TOKENS),
+                    stop=(side == PARTNERS),
                 )
+
+        def relu(j):
             pos_part = ring.tile([P, PACK, P], F32, name="pos_part", align_bytes=64)
-            src = pre[:].rearrange("s (p t) -> s t p", t=PACK)
+            src = bank_of[j][:].rearrange("s (p t) -> s t p", t=PACK)
             if j == GROUPS - 1:
                 for t in (0, 2):
                     nc.vector.tensor_scalar_max(pos_part[:, t : t + 2, :], src[:, t : t + 2, :], 0.0)
+            elif j == 5:
+                nc.vector.tensor_scalar_max(pos_part[:], src, 0.0)
             else:
                 nc.scalar.activation(pos_part[:], src, ACT.Relu)
             relu_of[j] = pos_part
+
+        def first_layer(j):
+            sums(j)
+            relu(j)
 
         def turn_and_square(j):
             turned = ps_turn.tile([P, PACK, P], F32, name="turned")
@@ -163,18 +154,34 @@ def tile_moe_duo_relu2_kernel(
                 nc.tensor.transpose(turned[:, t, :], relu_of[j][:, t, :], ident[:])
             nc.scalar.activation(hb[:, j * P : (j + 1) * P, :], turned[:].rearrange("p t s -> p s t"), ACT.Square)
 
-        gather(TOKENS, 0, first_count[TOKENS])
-        gather_sort(WORDS, PARTNERS, 0, first_count[PARTNERS])
-        gather_sort(SCALES, PARTNERS, 0, 1)
-        gather_sort(SCALES, PARTNERS, 1, first_count[PARTNERS] - 1)
-        for j in range(GROUPS):
-            first_layer(j)
-            for piece in gathers_behind.get(j, ()):
-                gather(*piece)
-            if j > 0:
-                turn_and_square(j - 1)
-        turn_and_square(GROUPS - 1)
+        gather(WORDS, 0, 3)
+        gather(SCALES, 0, 1)
+        gather(SCALES, 1, 2)
+        gather(SCALES, 3, 2)
+        first_layer(0)
+        gather(WORDS, 3, 2)
+        first_layer(1)
+        gather(SCALES, 5, 2)
+        first_layer(2)
+        gather(WORDS, 5, 2)
+        turn_and_square(0)
+        turn_and_square(1)
+        first_layer(3)
+        gather(SCALES, 7, 1)
+        first_layer(4)
+        turn_and_square(2)
+        turn_and_square(3)
+        first_layer(5)
+        gather(WORDS, 7, 1)
+        first_layer(6)
+        turn_and_square(4)
+        turn_and_square(5)
+        first_layer(7)
+        turn_and_square(6)
+        turn_and_square(7)
 
+        hw = keep.tile([P, S], U32, name="hw", tag="xw", align_bytes=64)
+        hs = keep.tile([P, S], U8, name="hs", align_bytes=64)
         y = keep.tile([P, S], F32, name="y", align_bytes=64)
 
         def quantize(a, b):
@@ -192,22 +199,21 @@ def tile_moe_duo_relu2_kernel(
                 stop=True,
             )
 
-        bank_first = bank_of(GROUPS - 2)
-        bank_mid = ps_keep.tile([P, H], F32, name="bank_mid")
         bank_last = ps_keep.tile([P, H], F32, name="bank_last")
-        mid, last = 2 * C, S - P
+        mid, third, last = 2 * C, 3 * C, S - P
         quantize(0, C)
         quantize(C, mid)
-        second_layer(bank_first, 0, 0, C)
-        second_layer(bank_first, 0, C, mid)
-        quantize(mid, mid + C)
-        nc.vector.tensor_copy(y[:, 0:mid], bank_first[:])
-        second_layer(bank_mid, mid, mid, mid + C)
-        quantize(mid + C, last)
-        second_layer(bank_mid, mid, mid + C, last)
+        second_layer(pre_banks[1], 0, 0, C)
+        second_layer(pre_banks[1], 0, C, mid)
+        quantize(mid, third)
+        second_layer(pre_banks[0], mid, mid, third)
+        quantize(third, last)
+        second_layer(pre_banks[2], third, third, last)
+        nc.vector.tensor_copy(y[:, mid:third], pre_banks[0][:, 0:C])
         quantize(last, S)
         second_layer(bank_last, last, last, S)
-        nc.scalar.copy(y[:, mid:last], bank_mid[:, 0 : last - mid])
+        nc.scalar.copy(y[:, 0:mid], pre_banks[1][:])
+        nc.scalar.copy(y[:, third:last], pre_banks[2][:, 0:P])
         nc.scalar.copy(y[:, last:S], bank_last[:, 0:P])
 
         part1 = keep.tile([P, T], F32, name="part1", align_bytes=64)

@@ -32,18 +32,17 @@ def tile_moe_duo_relu2_kernel(
     nc = tc.nc
     with ExitStack() as ctx:
         keep = ctx.enter_context(tc.tile_pool(name="keep", bufs=1))
-        ring = ctx.enter_context(tc.tile_pool(name="ring", bufs=4))
+        ring = ctx.enter_context(tc.tile_pool(name="ring", bufs=5))
         ps_keep = ctx.enter_context(tc.psum_pool(name="ps_keep", bufs=1))
-        ps_turn = ctx.enter_context(tc.psum_pool(name="ps_turn", bufs=3))
 
         tok_list = keep.tile([P, S // LIST_ROWS], U16, name="tok_list")
         par_list = keep.tile([P, S // LIST_ROWS], U16, name="par_list")
         pos1_list = keep.tile([P, T // LIST_ROWS], U16, name="pos1_list")
         pos2_list = keep.tile([P, T // LIST_ROWS], U16, name="pos2_list")
-        xw = keep.tile([P, T], I32, name="xw", tag="xw", align_bytes=64)
+        xw = keep.tile([P, T], I32, name="xw", align_bytes=64)
         xs = keep.tile([P, T], U8, name="xs", align_bytes=64)
         w1w = keep.tile([P, E, 2 * H], U8, name="w1w", align_bytes=64)
-        wpw = keep.tile([P, E, 2 * H], U8, name="wpw", align_bytes=64)
+        wpw = keep.tile([P, E, 2 * H], U8, name="wpw", tag="wpw", align_bytes=64)
         w2w = keep.tile([P, E, 2 * N], U8, name="w2w", align_bytes=64)
         w1s_pad = keep.tile([P, E * H + 4], U8, name="w1s_pad", align_bytes=64)
         wps_pad = keep.tile([P, E * H + 4], U8, name="wps_pad", align_bytes=64)
@@ -80,10 +79,10 @@ def tile_moe_duo_relu2_kernel(
         load_x_scales(nc.sync, (0, 1))
         load_words(nc.scalar, w1w, w1_words, 0, 1)
         make_identity(nc, ident[:])
-        pre_banks = [ps_keep.tile([P, H], F32, name="pre%d" % i) for i in range(3)]
+        banks = [ps_keep.tile([P, H], F32, name="bank%d" % i) for i in range(8)]
         load_scales(nc.sync, w1s, w1_scales)
         load_scales(nc.scalar, wps, wp_scales)
-        for e0, e1 in ((1, 2), (2, E)):
+        for e0, e1 in ((1, 3), (3, E)):
             load_words(nc.sync, w1w, w1_words, e0, e1)
             load_words(nc.sync, wpw, wp_words, e0, e1)
         load_words(nc.sync, w2w, w2_words, 0, E)
@@ -92,17 +91,17 @@ def tile_moe_duo_relu2_kernel(
         nc.sync.dma_start(pos2_list[:], pos2)
         nc.sync.dma_start(gates[:], gate.rearrange("r p t -> p r t"))
 
-        tok_w = keep.tile([P, 4 * P], U32, name="tok_w", align_bytes=64)
-        par_w = keep.tile([P, 4 * P], U32, name="par_w", align_bytes=64)
-        tok_s = keep.tile([P, 5 * P], U8, name="tok_s", align_bytes=64)
-        par_s = keep.tile([P, 5 * P], U8, name="par_s", align_bytes=64)
+        tok_w = keep.tile([P, 5 * P], U32, name="tok_w", align_bytes=64)
+        par_w = keep.tile([P, 5 * P], U32, name="par_w", align_bytes=64)
+        tok_s = keep.tile([P, 4 * P], U8, name="tok_s", align_bytes=64)
+        par_s = keep.tile([P, 4 * P], U8, name="par_s", align_bytes=64)
 
         windows = (xw[:].bitcast(U32), xs[:])
         gathered = ((tok_w, tok_s), (par_w, par_s))
         lists = (tok_list, par_list)
         weights = ((w1w, w1s), (wpw, wps))
 
-        places = ((1, 2, 3, 0, 1, 2, 3, 2), (0, 1, 2, 3, 4, 0, 1, 3))
+        places = ([(j + 2) % 5 for j in range(GROUPS)], [j % 4 for j in range(GROUPS)])
 
         def gather_side(sort, side, j, count):
             cols = slice(places[sort][j] * P, (places[sort][j] + count) * P)
@@ -115,7 +114,8 @@ def tile_moe_duo_relu2_kernel(
 
         hb = keep.tile([P, S, PACK], BF16, name="hb", align_bytes=64)
         relu_of = {}
-        bank_of = [pre_banks[i] for i in (0, 1, 2, 1, 0, 1, 2, 1)]
+        bank_of = [banks[i] for i in (0, 1, 2, 1, 0, 2, 2, 5)]
+        turn_of = [banks[i] for i in (3, 4, 5, 3, 4, 6, 0, 1)]
 
         def sums(j):
             e = j * P // C
@@ -138,7 +138,7 @@ def tile_moe_duo_relu2_kernel(
             if j == GROUPS - 1:
                 for t in (0, 2):
                     nc.vector.tensor_scalar_max(pos_part[:, t : t + 2, :], src[:, t : t + 2, :], 0.0)
-            elif j == 5:
+            elif j == GROUPS - 2:
                 nc.vector.tensor_scalar_max(pos_part[:], src, 0.0)
             else:
                 nc.scalar.activation(pos_part[:], src, ACT.Relu)
@@ -149,38 +149,35 @@ def tile_moe_duo_relu2_kernel(
             relu(j)
 
         def turn_and_square(j):
-            turned = ps_turn.tile([P, PACK, P], F32, name="turned")
+            turned = turn_of[j][:].rearrange("p (t s) -> p t s", t=PACK)
             for t in range(PACK):
                 nc.tensor.transpose(turned[:, t, :], relu_of[j][:, t, :], ident[:])
-            nc.scalar.activation(hb[:, j * P : (j + 1) * P, :], turned[:].rearrange("p t s -> p s t"), ACT.Square)
+            nc.scalar.activation(hb[:, j * P : (j + 1) * P, :], turned.rearrange("p t s -> p s t"), ACT.Square)
 
         gather(WORDS, 0, 3)
         gather(SCALES, 0, 1)
-        gather(SCALES, 1, 2)
-        gather(SCALES, 3, 2)
+        gather(SCALES, 1, 3)
         first_layer(0)
-        gather(WORDS, 3, 2)
+        gather(WORDS, 3, 3)
         first_layer(1)
-        gather(SCALES, 5, 2)
+        gather(SCALES, 4, 2)
         first_layer(2)
-        gather(WORDS, 5, 2)
+        gather(WORDS, 6, 2)
+        gather(SCALES, 6, 1)
         turn_and_square(0)
         turn_and_square(1)
         first_layer(3)
         gather(SCALES, 7, 1)
         first_layer(4)
-        turn_and_square(2)
-        turn_and_square(3)
         first_layer(5)
-        gather(WORDS, 7, 1)
+        for j in range(2, 6):
+            turn_and_square(j)
         first_layer(6)
-        turn_and_square(4)
-        turn_and_square(5)
         first_layer(7)
         turn_and_square(6)
         turn_and_square(7)
 
-        hw = keep.tile([P, S], U32, name="hw", tag="xw", align_bytes=64)
+        hw = keep.tile([P, S], U32, name="hw", tag="wpw", align_bytes=64)
         hs = keep.tile([P, S], U8, name="hs", align_bytes=64)
         y = keep.tile([P, S], F32, name="y", align_bytes=64)
 
@@ -199,22 +196,19 @@ def tile_moe_duo_relu2_kernel(
                 stop=True,
             )
 
-        bank_last = ps_keep.tile([P, H], F32, name="bank_last")
         mid, third, last = 2 * C, 3 * C, S - P
-        quantize(0, C)
-        quantize(C, mid)
-        second_layer(pre_banks[1], 0, 0, C)
-        second_layer(pre_banks[1], 0, C, mid)
+        quantize(0, mid)
+        second_layer(banks[5], 0, 0, C)
+        second_layer(banks[5], 0, C, mid)
         quantize(mid, third)
-        second_layer(pre_banks[0], mid, mid, third)
+        second_layer(banks[2], mid, mid, third)
         quantize(third, last)
-        second_layer(pre_banks[2], third, third, last)
-        nc.vector.tensor_copy(y[:, mid:third], pre_banks[0][:, 0:C])
+        second_layer(banks[2], mid, third, last)
         quantize(last, S)
-        second_layer(bank_last, last, last, S)
-        nc.scalar.copy(y[:, 0:mid], pre_banks[1][:])
-        nc.scalar.copy(y[:, third:last], pre_banks[2][:, 0:P])
-        nc.scalar.copy(y[:, last:S], bank_last[:, 0:P])
+        second_layer(banks[7], last, last, S)
+        nc.scalar.copy(y[:, 0:mid], banks[5][:])
+        nc.scalar.copy(y[:, mid:last], banks[2][:, 0 : last - mid])
+        nc.vector.tensor_copy(y[:, last:S], banks[7][:, 0:P])
 
         part1 = keep.tile([P, T], F32, name="part1", align_bytes=64)
         part2 = keep.tile([P, T], F32, name="part2", align_bytes=64)

@@ -71,17 +71,16 @@ def tile_moe_duo_relu2_kernel(
             for r in rows:
                 queue.dma_start(xs[r:P:32, :].bitcast(I32), xs_rows[r].bitcast(I32))
 
+        nc.sync.dma_start(xw[:], x_words[0].rearrange("p t d -> p (t d)").bitcast(I32))
         nc.sync.dma_start(tok_list[:], offs)
-        nc.scalar.dma_start(xw[:], x_words[0].rearrange("p t d -> p (t d)").bitcast(I32))
         load_words(nc.gpsimd, wpw, wp_words, 0, 1)
         nc.sync.dma_start(par_list[:], offs2)
-        load_x_scales(nc.scalar, (2, 3))
-        load_x_scales(nc.sync, (0, 1))
-        load_words(nc.scalar, w1w, w1_words, 0, 1)
+        load_x_scales(nc.scalar, range(PACK))
+        load_words(nc.sync, w1w, w1_words, 0, 1)
         make_identity(nc, ident[:])
         banks = [ps_keep.tile([P, H], F32, name="bank%d" % i) for i in range(8)]
         load_scales(nc.sync, w1s, w1_scales)
-        load_scales(nc.scalar, wps, wp_scales)
+        load_scales(nc.sync, wps, wp_scales)
         for e0, e1 in ((1, 3), (3, E)):
             load_words(nc.sync, w1w, w1_words, e0, e1)
             load_words(nc.sync, wpw, wp_words, e0, e1)
@@ -114,8 +113,8 @@ def tile_moe_duo_relu2_kernel(
 
         hb = keep.tile([P, S, PACK], BF16, name="hb", align_bytes=64)
         relu_of = {}
-        bank_of = [banks[i] for i in (0, 1, 2, 1, 0, 2, 2, 5)]
-        turn_of = [banks[i] for i in (3, 4, 5, 3, 4, 6, 0, 1)]
+        bank_of = [banks[i] for i in (0, 1, 2, 1, 0, 2, 0, 2)]
+        turn_of = [banks[i] for i in (3, 4, 5, 3, 4, 5, 6, 1)]
 
         def sums(j):
             e = j * P // C
@@ -155,8 +154,8 @@ def tile_moe_duo_relu2_kernel(
             nc.scalar.activation(hb[:, j * P : (j + 1) * P, :], turned.rearrange("p t s -> p s t"), ACT.Square)
 
         gather(WORDS, 0, 3)
-        gather(SCALES, 0, 1)
-        gather(SCALES, 1, 3)
+        gather(SCALES, 0, 2)
+        gather(SCALES, 2, 2)
         first_layer(0)
         gather(WORDS, 3, 3)
         first_layer(1)
@@ -170,10 +169,11 @@ def tile_moe_duo_relu2_kernel(
         gather(SCALES, 7, 1)
         first_layer(4)
         first_layer(5)
-        for j in range(2, 6):
+        for j in range(2, 5):
             turn_and_square(j)
         first_layer(6)
         first_layer(7)
+        turn_and_square(5)
         turn_and_square(6)
         turn_and_square(7)
 
@@ -198,16 +198,16 @@ def tile_moe_duo_relu2_kernel(
 
         mid, third, last = 2 * C, 3 * C, S - P
         quantize(0, mid)
-        second_layer(banks[5], 0, 0, C)
-        second_layer(banks[5], 0, C, mid)
+        second_layer(banks[2], 0, 0, C)
+        second_layer(banks[2], 0, C, mid)
         quantize(mid, third)
-        second_layer(banks[2], mid, mid, third)
+        second_layer(banks[0], mid, mid, third)
         quantize(third, last)
-        second_layer(banks[2], mid, third, last)
+        second_layer(banks[0], mid, third, last)
         quantize(last, S)
         second_layer(banks[7], last, last, S)
-        nc.scalar.copy(y[:, 0:mid], banks[5][:])
-        nc.scalar.copy(y[:, mid:last], banks[2][:, 0 : last - mid])
+        nc.scalar.copy(y[:, 0:mid], banks[2][:])
+        nc.scalar.copy(y[:, mid:last], banks[0][:, 0 : last - mid])
         nc.vector.tensor_copy(y[:, last:S], banks[7][:, 0:P])
 
         part1 = keep.tile([P, T], F32, name="part1", align_bytes=64)

@@ -14,6 +14,13 @@ LIST_ROWS = 16
 TOKENS, PARTNERS = 0, 1
 WORDS, SCALES = 0, 1
 
+RUN = 3
+RUNS = [range(j, min(j + RUN, GROUPS)) for j in range(0, GROUPS, RUN)]
+SCALE_PIECES = [range(0, 2), range(2, 5), range(5, 7), range(7, 8)]
+PLACES = 6
+PLACE = ((3, 4, 5, 1, 2, 3, 0, 1), (4, 5, 1, 2, 3, 0, 1, 2))
+BANK_FROM = {3: 1, 4: 0, 5: 2, 6: 4, 7: 5}
+
 F32 = mybir.dt.float32
 BF16 = mybir.dt.bfloat16
 I32 = mybir.dt.int32
@@ -32,7 +39,7 @@ def tile_moe_duo_relu2_kernel(
     nc = tc.nc
     with ExitStack() as ctx:
         keep = ctx.enter_context(tc.tile_pool(name="keep", bufs=1))
-        ring = ctx.enter_context(tc.tile_pool(name="ring", bufs=5))
+        ring = ctx.enter_context(tc.tile_pool(name="ring", bufs=RUN + 2))
         ps_keep = ctx.enter_context(tc.psum_pool(name="ps_keep", bufs=1))
 
         tok_list = keep.tile([P, S // LIST_ROWS], U16, name="tok_list")
@@ -56,75 +63,76 @@ def tile_moe_duo_relu2_kernel(
         for scale_tile in (xs, w1s_pad, wps_pad, w2s_pad):
             nc.vector.memset(scale_tile[:].bitcast(I32), 0)
 
-        def load_scales(queue, scale_tile, src):
+        def load_scales(scale_tile, src):
             by_row = src.rearrange("e s (q r) c -> r q (e s) c", r=PACK)
             for r in range(PACK):
                 dst = scale_tile[r:P:32, :].bitcast(I32).rearrange("q (e c) -> q e c", e=E)
-                queue.dma_start(dst, by_row[r].bitcast(I32))
+                nc.sync.dma_start(dst, by_row[r].bitcast(I32))
 
         def load_words(queue, tile, src, e0, e1):
             queue.dma_start(tile[:, e0:e1, :].bitcast(I32), src[e0:e1, 0].rearrange("e p c -> p e c").bitcast(I32))
-
-        xs_rows = x_scales[0].rearrange("(q r) c -> r q c", r=PACK)
-
-        def load_x_scales(queue, rows):
-            for r in rows:
-                queue.dma_start(xs[r:P:32, :].bitcast(I32), xs_rows[r].bitcast(I32))
 
         nc.sync.dma_start(xw[:], x_words[0].rearrange("p t d -> p (t d)").bitcast(I32))
         nc.sync.dma_start(tok_list[:], offs)
         load_words(nc.gpsimd, wpw, wp_words, 0, 1)
         nc.sync.dma_start(par_list[:], offs2)
-        load_x_scales(nc.scalar, range(PACK))
+        xs_rows = x_scales[0].rearrange("(q r) c -> r q c", r=PACK)
+        for r in range(PACK):
+            nc.scalar.dma_start(xs[r:P:32, :].bitcast(I32), xs_rows[r].bitcast(I32))
         load_words(nc.sync, w1w, w1_words, 0, 1)
         make_identity(nc, ident[:])
-        banks = [ps_keep.tile([P, H], F32, name="bank%d" % i) for i in range(8)]
-        load_scales(nc.sync, w1s, w1_scales)
-        load_scales(nc.sync, wps, wp_scales)
-        for e0, e1 in ((1, 3), (3, E)):
+        load_scales(w1s, w1_scales)
+        load_scales(wps, wp_scales)
+        for e0, e1 in ((1, E - 1), (E - 1, E)):
             load_words(nc.sync, w1w, w1_words, e0, e1)
             load_words(nc.sync, wpw, wp_words, e0, e1)
         load_words(nc.sync, w2w, w2_words, 0, E)
-        load_scales(nc.sync, w2s, w2_scales)
+        load_scales(w2s, w2_scales)
         nc.sync.dma_start(pos1_list[:], pos1)
         nc.sync.dma_start(pos2_list[:], pos2)
         nc.sync.dma_start(gates[:], gate.rearrange("r p t -> p r t"))
 
-        tok_w = keep.tile([P, 5 * P], U32, name="tok_w", align_bytes=64)
-        par_w = keep.tile([P, 5 * P], U32, name="par_w", align_bytes=64)
-        tok_s = keep.tile([P, 4 * P], U8, name="tok_s", align_bytes=64)
-        par_s = keep.tile([P, 4 * P], U8, name="par_s", align_bytes=64)
+        tok_w = keep.tile([P, PLACES * P], U32, name="tok_w", align_bytes=64)
+        par_w = keep.tile([P, PLACES * P], U32, name="par_w", align_bytes=64)
+        tok_s = keep.tile([P, PLACES * P], U8, name="tok_s", align_bytes=64)
+        par_s = keep.tile([P, PLACES * P], U8, name="par_s", align_bytes=64)
 
         windows = (xw[:].bitcast(U32), xs[:])
         gathered = ((tok_w, tok_s), (par_w, par_s))
         lists = (tok_list, par_list)
         weights = ((w1w, w1s), (wpw, wps))
 
-        places = ([(j + 2) % 5 for j in range(GROUPS)], [j % 4 for j in range(GROUPS)])
+        def columns(sort, groups):
+            return slice(PLACE[sort][groups[0]] * P, (PLACE[sort][groups[-1]] + 1) * P)
 
-        def gather_side(sort, side, j, count):
-            cols = slice(places[sort][j] * P, (places[sort][j] + count) * P)
-            offsets = lists[side][:, j * P // LIST_ROWS : (j + count) * P // LIST_ROWS]
-            nc.vector.tensor_copy(gathered[side][sort][:, cols], windows[sort].indirect(offsets))
+        def gather(sort, groups):
+            for side in (TOKENS, PARTNERS):
+                offsets = lists[side][:, groups[0] * P // LIST_ROWS : (groups[-1] + 1) * P // LIST_ROWS]
+                nc.vector.tensor_copy(gathered[side][sort][:, columns(sort, groups)], windows[sort].indirect(offsets))
 
-        def gather(sort, j, count):
-            gather_side(sort, TOKENS, j, count)
-            gather_side(sort, PARTNERS, j, count)
+        gathers_behind = {}
+        for sort, pieces in ((WORDS, RUNS), (SCALES, SCALE_PIECES)):
+            for groups in pieces:
+                taken = [PLACE[sort][j] for j in groups]
+                holder = max([-1] + [j for j in range(groups[0]) if PLACE[sort][j] in taken])
+                gathers_behind.setdefault(holder, []).append((sort, groups))
+
+        sum_bank = [ps_keep.tile([P, H], F32, name="sum%d" % j) for j in range(RUN)]
+        for j in range(RUN, GROUPS):
+            sum_bank.append(sum_bank[BANK_FROM[j]])
+        turn_banks = [ps_keep.tile([P, PACK, P], F32, name="turn%d" % i) for i in range(RUN)]
+        last_bank = ps_keep.tile([P, P], F32, name="last_bank")
 
         hb = keep.tile([P, S, PACK], BF16, name="hb", align_bytes=64)
         relu_of = {}
-        bank_of = [banks[i] for i in (0, 1, 2, 1, 0, 2, 0, 2)]
-        turn_of = [banks[i] for i in (3, 4, 5, 3, 4, 5, 6, 1)]
 
-        def sums(j):
+        def first_sum(j):
             e = j * P // C
             for side in (TOKENS, PARTNERS):
-                wcols = slice(places[WORDS][j] * P, (places[WORDS][j] + 1) * P)
-                scols = slice(places[SCALES][j] * P, (places[SCALES][j] + 1) * P)
                 nc.tensor.matmul_mx(
-                    bank_of[j][:],
-                    lhsT=gathered[side][WORDS][:, wcols].bitcast(FP8X4),
-                    lhsT_scale=gathered[side][SCALES][:, scols],
+                    sum_bank[j][:],
+                    lhsT=gathered[side][WORDS][:, columns(WORDS, [j])].bitcast(FP8X4),
+                    lhsT_scale=gathered[side][SCALES][:, columns(SCALES, [j])],
                     rhs=weights[side][WORDS][:, e, :].bitcast(FP4X4),
                     rhs_scale=weights[side][SCALES][:, e * H : (e + 1) * H],
                     start=(side == TOKENS),
@@ -133,49 +141,37 @@ def tile_moe_duo_relu2_kernel(
 
         def relu(j):
             pos_part = ring.tile([P, PACK, P], F32, name="pos_part", align_bytes=64)
-            src = bank_of[j][:].rearrange("s (p t) -> s t p", t=PACK)
-            if j == GROUPS - 1:
-                for t in (0, 2):
-                    nc.vector.tensor_scalar_max(pos_part[:, t : t + 2, :], src[:, t : t + 2, :], 0.0)
-            elif j == GROUPS - 2:
-                nc.vector.tensor_scalar_max(pos_part[:], src, 0.0)
-            else:
+            src = sum_bank[j][:].rearrange("s (p t) -> s t p", t=PACK)
+            if j not in RUNS[-1]:
                 nc.scalar.activation(pos_part[:], src, ACT.Relu)
+            else:
+                step = PACK // 2 if j == GROUPS - 1 else PACK
+                for t in range(0, PACK, step):
+                    nc.vector.tensor_scalar_max(pos_part[:, t : t + step, :], src[:, t : t + step, :], 0.0)
             relu_of[j] = pos_part
 
-        def first_layer(j):
-            sums(j)
-            relu(j)
-
-        def turn_and_square(j):
-            turned = turn_of[j][:].rearrange("p (t s) -> p t s", t=PACK)
+        def turn(j):
+            turned = turn_banks[j % RUN]
             for t in range(PACK):
                 nc.tensor.transpose(turned[:, t, :], relu_of[j][:, t, :], ident[:])
-            nc.scalar.activation(hb[:, j * P : (j + 1) * P, :], turned.rearrange("p t s -> p s t"), ACT.Square)
+            step = P // 2 if j == GROUPS - 1 else P
+            for s0 in range(0, P, step):
+                src = turned[:, :, s0 : s0 + step].rearrange("p t s -> p s t")
+                nc.scalar.activation(hb[:, j * P + s0 : j * P + s0 + step, :], src, ACT.Square)
 
-        gather(WORDS, 0, 3)
-        gather(SCALES, 0, 2)
-        gather(SCALES, 2, 2)
-        first_layer(0)
-        gather(WORDS, 3, 3)
-        first_layer(1)
-        gather(SCALES, 4, 2)
-        first_layer(2)
-        gather(WORDS, 6, 2)
-        gather(SCALES, 6, 1)
-        turn_and_square(0)
-        turn_and_square(1)
-        first_layer(3)
-        gather(SCALES, 7, 1)
-        first_layer(4)
-        first_layer(5)
-        for j in range(2, 5):
-            turn_and_square(j)
-        first_layer(6)
-        first_layer(7)
-        turn_and_square(5)
-        turn_and_square(6)
-        turn_and_square(7)
+        for piece in gathers_behind[-1]:
+            gather(*piece)
+        turned_up_to = 0
+        for run in RUNS:
+            for j in run:
+                first_sum(j)
+                relu(j)
+                for piece in gathers_behind.get(j, ()):
+                    gather(*piece)
+            stop = GROUPS if run == RUNS[-1] else run[-1]
+            for j in range(turned_up_to, stop):
+                turn(j)
+            turned_up_to = stop
 
         hw = keep.tile([P, S], U32, name="hw", tag="wpw", align_bytes=64)
         hs = keep.tile([P, S], U8, name="hs", align_bytes=64)
@@ -197,18 +193,20 @@ def tile_moe_duo_relu2_kernel(
             )
 
         mid, third, last = 2 * C, 3 * C, S - P
+        bank_first, bank_mid = sum_bank[GROUPS - 1], sum_bank[GROUPS - 2]
         quantize(0, mid)
-        second_layer(banks[2], 0, 0, C)
-        second_layer(banks[2], 0, C, mid)
+        second_layer(bank_first, 0, 0, C)
+        second_layer(bank_first, 0, C, mid)
         quantize(mid, third)
-        second_layer(banks[0], mid, mid, third)
+        second_layer(bank_mid, mid, mid, third)
         quantize(third, last)
-        second_layer(banks[0], mid, third, last)
-        quantize(last, S)
-        second_layer(banks[7], last, last, S)
-        nc.scalar.copy(y[:, 0:mid], banks[2][:])
-        nc.scalar.copy(y[:, mid:last], banks[0][:, 0 : last - mid])
-        nc.vector.tensor_copy(y[:, last:S], banks[7][:, 0:P])
+        second_layer(bank_mid, mid, third, last)
+        quantize(last, last + P // 2)
+        quantize(last + P // 2, S)
+        second_layer(last_bank, last, last, S)
+        nc.scalar.copy(y[:, 0:mid], bank_first[:])
+        nc.scalar.copy(y[:, mid:last], bank_mid[:, 0 : last - mid])
+        nc.vector.tensor_copy(y[:, last:S], last_bank[:])
 
         part1 = keep.tile([P, T], F32, name="part1", align_bytes=64)
         part2 = keep.tile([P, T], F32, name="part2", align_bytes=64)

@@ -19,7 +19,8 @@ RUNS = [range(j, min(j + RUN, GROUPS)) for j in range(0, GROUPS, RUN)]
 SCALE_PIECES = [range(0, 2), range(2, 5), range(5, 7), range(7, 8)]
 PLACES = 6
 PLACE = ((3, 4, 5, 1, 2, 3, 0, 1), (4, 5, 1, 2, 3, 0, 1, 2))
-BANK_FROM = {3: 1, 4: 0, 5: 2, 6: 4, 7: 5}
+BANK_FROM = {3: 1, 4: 0, 5: 2, 6: 5}
+LAST_EXPERT = range(GROUPS - C // P, GROUPS)
 
 F32 = mybir.dt.float32
 BF16 = mybir.dt.bfloat16
@@ -92,6 +93,16 @@ def tile_moe_duo_relu2_kernel(
         nc.sync.dma_start(pos2_list[:], pos2)
         nc.sync.dma_start(gates[:], gate.rearrange("r p t -> p r t"))
 
+        last_w = [keep.tile([P, PACK, 2 * P], U8, name="last_w%d" % side, tag="last_w%d" % side, align_bytes=64) for side in (TOKENS, PARTNERS)]
+        last_s = [keep.tile([P, PACK, P], U8, name="last_s%d" % side, align_bytes=64) for side in (TOKENS, PARTNERS)]
+        for side, scale_tile in ((TOKENS, w1s), (PARTNERS, wps)):
+            nc.gpsimd.tensor_copy(last_s[side][:], scale_tile[:, (E - 1) * H : E * H].rearrange("k (p t) -> k t p", t=PACK))
+        for side, words in ((TOKENS, w1w), (PARTNERS, wpw)):
+            nc.gpsimd.tensor_copy(
+                last_w[side][:].rearrange("k t (p b) -> k t p b", b=2),
+                words[:, E - 1, :].rearrange("k (p t b) -> k t p b", t=PACK, b=2),
+            )
+
         tok_w = keep.tile([P, PLACES * P], U32, name="tok_w", align_bytes=64)
         par_w = keep.tile([P, PLACES * P], U32, name="par_w", align_bytes=64)
         tok_s = keep.tile([P, PLACES * P], U8, name="tok_s", align_bytes=64)
@@ -118,13 +129,36 @@ def tile_moe_duo_relu2_kernel(
                 gathers_behind.setdefault(holder, []).append((sort, groups))
 
         sum_bank = [ps_keep.tile([P, H], F32, name="sum%d" % j) for j in range(RUN)]
-        for j in range(RUN, GROUPS):
+        for j in range(RUN, GROUPS - 1):
             sum_bank.append(sum_bank[BANK_FROM[j]])
-        turn_banks = [ps_keep.tile([P, PACK, P], F32, name="turn%d" % i) for i in range(RUN)]
+        turn_banks = [ps_keep.tile([P, H], F32, name="turn%d" % i) for i in range(RUN + 1)]
+        sum_bank.append(turn_banks[2])
+        turn_bank = (0, 1, 2, 0, 1, 3)
         last_bank = ps_keep.tile([P, P], F32, name="last_bank")
 
         hb = keep.tile([P, S, PACK], BF16, name="hb", align_bytes=64)
         relu_of = {}
+
+        def last_sum(j):
+            for side in (TOKENS, PARTNERS):
+                for t in range(PACK):
+                    nc.tensor.matmul_mx(
+                        sum_bank[j][:, t * P : (t + 1) * P],
+                        lhsT=last_w[side][:, t, :].bitcast(FP4X4),
+                        lhsT_scale=last_s[side][:, t, :],
+                        rhs=gathered[side][WORDS][:, columns(WORDS, [j])].bitcast(FP8X4),
+                        rhs_scale=gathered[side][SCALES][:, columns(SCALES, [j])],
+                        start=(side == TOKENS and t == 0),
+                        stop=(side == PARTNERS and t == PACK - 1),
+                    )
+
+        def relu_square(j):
+            pos_part = ring.tile([P, P, PACK], F32, name="pos_part", align_bytes=64)
+            src = sum_bank[j][:].rearrange("p (t s) -> p s t", t=PACK)
+            step = P // 2 if j == GROUPS - 1 else P
+            for s0 in range(0, P, step):
+                nc.vector.tensor_scalar_max(pos_part[:, s0 : s0 + step, :], src[:, s0 : s0 + step, :], 0.0)
+                nc.scalar.activation(hb[:, j * P + s0 : j * P + s0 + step, :], pos_part[:, s0 : s0 + step, :], ACT.Square)
 
         def first_sum(j):
             e = j * P // C
@@ -142,38 +176,34 @@ def tile_moe_duo_relu2_kernel(
         def relu(j):
             pos_part = ring.tile([P, PACK, P], F32, name="pos_part", align_bytes=64)
             src = sum_bank[j][:].rearrange("s (p t) -> s t p", t=PACK)
-            if j not in RUNS[-1]:
-                nc.scalar.activation(pos_part[:], src, ACT.Relu)
-            else:
-                step = PACK // 2 if j == GROUPS - 1 else PACK
-                for t in range(0, PACK, step):
-                    nc.vector.tensor_scalar_max(pos_part[:, t : t + step, :], src[:, t : t + step, :], 0.0)
+            nc.scalar.activation(pos_part[:], src, ACT.Relu)
             relu_of[j] = pos_part
 
         def turn(j):
-            turned = turn_banks[j % RUN]
+            turned = turn_banks[turn_bank[j]][:].rearrange("p (t s) -> p t s", t=PACK)
             for t in range(PACK):
                 nc.tensor.transpose(turned[:, t, :], relu_of[j][:, t, :], ident[:])
-            step = P // 2 if j == GROUPS - 1 else P
-            for s0 in range(0, P, step):
-                src = turned[:, :, s0 : s0 + step].rearrange("p t s -> p s t")
-                nc.scalar.activation(hb[:, j * P + s0 : j * P + s0 + step, :], src, ACT.Square)
+            nc.scalar.activation(hb[:, j * P : (j + 1) * P, :], turned.rearrange("p t s -> p s t"), ACT.Square)
 
         for piece in gathers_behind[-1]:
             gather(*piece)
         turned_up_to = 0
-        for run in RUNS:
+        for run in RUNS[:-1]:
             for j in run:
                 first_sum(j)
                 relu(j)
                 for piece in gathers_behind.get(j, ()):
                     gather(*piece)
-            stop = GROUPS if run == RUNS[-1] else run[-1]
+            stop = run[-1] + 1 if run == RUNS[-2] else run[-1]
             for j in range(turned_up_to, stop):
                 turn(j)
             turned_up_to = stop
+        for j in LAST_EXPERT:
+            last_sum(j)
+        for j in LAST_EXPERT:
+            relu_square(j)
 
-        hw = keep.tile([P, S], U32, name="hw", tag="wpw", align_bytes=64)
+        hw = keep.tile([P, S], U32, name="hw", tag="last_w1", align_bytes=64)
         hs = keep.tile([P, S], U8, name="hs", align_bytes=64)
         y = keep.tile([P, S], F32, name="y", align_bytes=64)
 

@@ -19,7 +19,8 @@ RUNS = [range(j, min(j + RUN, GROUPS)) for j in range(0, GROUPS, RUN)]
 SCALE_PIECES = [range(0, 2), range(2, 5), range(5, 7), range(7, 8)]
 PLACES = 6
 PLACE = ((3, 4, 5, 1, 2, 3, 0, 1), (4, 5, 1, 2, 3, 0, 1, 2))
-BANK_FROM = {3: 1, 4: 0, 5: 2, 6: 5}
+STEPS = (((0, 1, 2), (0, 1)), ((3, 4), (2, 3)), ((5, 6, 7), (5, 4)))
+LAST_TURN = 4
 LAST_EXPERT = range(GROUPS - C // P, GROUPS)
 
 F32 = mybir.dt.float32
@@ -47,8 +48,8 @@ def tile_moe_duo_relu2_kernel(
         par_list = keep.tile([P, S // LIST_ROWS], U16, name="par_list")
         pos1_list = keep.tile([P, T // LIST_ROWS], U16, name="pos1_list")
         pos2_list = keep.tile([P, T // LIST_ROWS], U16, name="pos2_list")
-        xw = keep.tile([P, T], I32, name="xw", align_bytes=64)
-        xs = keep.tile([P, T], U8, name="xs", align_bytes=64)
+        xw = keep.tile([P, T], I32, name="xw", tag="xw", align_bytes=64)
+        xs = keep.tile([P, T], U8, name="xs", tag="xs", align_bytes=64)
         w1w = keep.tile([P, E, 2 * H], U8, name="w1w", align_bytes=64)
         wpw = keep.tile([P, E, 2 * H], U8, name="wpw", tag="wpw", align_bytes=64)
         w2w = keep.tile([P, E, 2 * N], U8, name="w2w", align_bytes=64)
@@ -82,8 +83,8 @@ def tile_moe_duo_relu2_kernel(
             nc.scalar.dma_start(xs[r:P:32, :].bitcast(I32), xs_rows[r].bitcast(I32))
         load_words(nc.sync, w1w, w1_words, 0, 1)
         make_identity(nc, ident[:])
-        load_scales(w1s, w1_scales)
         load_scales(wps, wp_scales)
+        load_scales(w1s, w1_scales)
         for e0, e1 in ((1, E - 1), (E - 1, E)):
             load_words(nc.sync, w1w, w1_words, e0, e1)
             load_words(nc.sync, wpw, wp_words, e0, e1)
@@ -128,13 +129,10 @@ def tile_moe_duo_relu2_kernel(
                 holder = max([-1] + [j for j in range(groups[0]) if PLACE[sort][j] in taken])
                 gathers_behind.setdefault(holder, []).append((sort, groups))
 
-        sum_bank = [ps_keep.tile([P, H], F32, name="sum%d" % j) for j in range(RUN)]
-        for j in range(RUN, GROUPS - 1):
-            sum_bank.append(sum_bank[BANK_FROM[j]])
-        turn_banks = [ps_keep.tile([P, H], F32, name="turn%d" % i) for i in range(RUN + 1)]
-        sum_bank.append(turn_banks[2])
-        turn_bank = (0, 1, 2, 0, 1, 3)
-        last_bank = ps_keep.tile([P, P], F32, name="last_bank")
+        banks = [ps_keep.tile([P, H], F32, name="bank%d" % i) for i in range(6)]
+        sum_bank = [banks[i] for i in (0, 1, 2, 2, 3, 3, 4, 0)]
+        turn_bank = [banks[i] for i in (3, 4, 4, 0, 3, 1)]
+        last_bank = banks[5]
 
         hb = keep.tile([P, S, PACK], BF16, name="hb", align_bytes=64)
         relu_of = {}
@@ -157,8 +155,9 @@ def tile_moe_duo_relu2_kernel(
             src = sum_bank[j][:].rearrange("p (t s) -> p s t", t=PACK)
             step = P // 2 if j == GROUPS - 1 else P
             for s0 in range(0, P, step):
-                nc.vector.tensor_scalar_max(pos_part[:, s0 : s0 + step, :], src[:, s0 : s0 + step, :], 0.0)
-                nc.scalar.activation(hb[:, j * P + s0 : j * P + s0 + step, :], pos_part[:, s0 : s0 + step, :], ACT.Square)
+                part = pos_part[:, s0 : s0 + step, :]
+                nc.scalar.activation(part, src[:, s0 : s0 + step, :], ACT.Relu)
+                nc.vector.tensor_tensor(hb[:, j * P + s0 : j * P + s0 + step, :], part, part, ALU.mult)
 
         def first_sum(j):
             e = j * P // C
@@ -180,31 +179,41 @@ def tile_moe_duo_relu2_kernel(
             relu_of[j] = pos_part
 
         def turn(j):
-            turned = turn_banks[turn_bank[j]][:].rearrange("p (t s) -> p t s", t=PACK)
+            turned = turn_bank[j][:].rearrange("p (t s) -> p t s", t=PACK)
             for t in range(PACK):
                 nc.tensor.transpose(turned[:, t, :], relu_of[j][:, t, :], ident[:])
-            nc.scalar.activation(hb[:, j * P : (j + 1) * P, :], turned.rearrange("p t s -> p s t"), ACT.Square)
+            step = P // 2 if j == LAST_TURN else P
+            for s0 in range(0, P, step):
+                src = turned[:, :, s0 : s0 + step].rearrange("p t s -> p s t")
+                nc.scalar.activation(hb[:, j * P + s0 : j * P + s0 + step, :], src, ACT.Square)
 
         for piece in gathers_behind[-1]:
             gather(*piece)
-        turned_up_to = 0
-        for run in RUNS[:-1]:
-            for j in run:
-                first_sum(j)
-                relu(j)
+        for i in range(3):
+            nc.tensor.matmul_mx(
+                last_bank[:],
+                lhsT=tok_w[:, columns(WORDS, [0])].bitcast(FP8X4),
+                lhsT_scale=w1w[:, 0, 0:P],
+                rhs=w1w[:, 0, :].bitcast(FP4X4),
+                rhs_scale=w1w[:, 0, 0:H],
+                start=True,
+                stop=True,
+            )
+        for sums, turns in STEPS:
+            for j in sums:
+                if j in LAST_EXPERT:
+                    last_sum(j)
+                    relu_square(j)
+                else:
+                    first_sum(j)
+                    relu(j)
                 for piece in gathers_behind.get(j, ()):
                     gather(*piece)
-            stop = run[-1] + 1 if run == RUNS[-2] else run[-1]
-            for j in range(turned_up_to, stop):
+            for j in turns:
                 turn(j)
-            turned_up_to = stop
-        for j in LAST_EXPERT:
-            last_sum(j)
-        for j in LAST_EXPERT:
-            relu_square(j)
 
-        hw = keep.tile([P, S], U32, name="hw", tag="last_w1", align_bytes=64)
-        hs = keep.tile([P, S], U8, name="hs", align_bytes=64)
+        hw = keep.tile([P, S], U32, name="hw", tag="xw", align_bytes=64)
+        hs = keep.tile([P, S], U8, name="hs", tag="xs", align_bytes=64)
         y = keep.tile([P, S], F32, name="y", align_bytes=64)
 
         def quantize(a, b):
@@ -222,21 +231,22 @@ def tile_moe_duo_relu2_kernel(
                 stop=True,
             )
 
-        mid, third, last = 2 * C, 3 * C, S - P
+        mid, third = 2 * C, 3 * C
+        late = mid + P
         bank_first, bank_mid = sum_bank[GROUPS - 1], sum_bank[GROUPS - 2]
         quantize(0, mid)
         second_layer(bank_first, 0, 0, C)
         second_layer(bank_first, 0, C, mid)
-        quantize(mid, third)
-        second_layer(bank_mid, mid, mid, third)
-        quantize(third, last)
-        second_layer(bank_mid, mid, third, last)
-        quantize(last, last + P // 2)
-        quantize(last + P // 2, S)
-        second_layer(last_bank, last, last, S)
+        quantize(third, S)
+        second_layer(bank_mid, late, third, S)
+        quantize(late, third)
+        second_layer(bank_mid, late, late, third)
+        quantize(mid, mid + P // 2)
+        quantize(mid + P // 2, late)
+        second_layer(last_bank, mid, mid, late)
         nc.scalar.copy(y[:, 0:mid], bank_first[:])
-        nc.scalar.copy(y[:, mid:last], bank_mid[:, 0 : last - mid])
-        nc.vector.tensor_copy(y[:, last:S], last_bank[:])
+        nc.vector.tensor_copy(y[:, late:S], bank_mid[:, 0 : S - late])
+        nc.scalar.copy(y[:, mid:late], last_bank[:, 0:P])
 
         part1 = keep.tile([P, T], F32, name="part1", align_bytes=64)
         part2 = keep.tile([P, T], F32, name="part2", align_bytes=64)

@@ -16,11 +16,12 @@ WORDS, SCALES = 0, 1
 
 RUN = 3
 RUNS = [range(j, min(j + RUN, GROUPS)) for j in range(0, GROUPS, RUN)]
-SCALE_PIECES = [range(0, 2), range(2, 5), range(5, 7), range(7, 8)]
-PLACES = 6
-PLACE = ((3, 4, 5, 1, 2, 3, 0, 1), (4, 5, 1, 2, 3, 0, 1, 2))
+SCALE_PIECES = [range(0, 2), range(2, 4), range(4, 6), range(6, 8)]
+WORD_PIECES = [range(0, 3), range(3, 5), range(5, 7), range(7, 8)]
+PLACES = 4
+PLACE = ((1, 2, 3, 0, 1, 2, 3, 1), (0, 1, 2, 3, 0, 1, 2, 3))
 STEPS = (((0, 1, 2), (0, 1)), ((3, 4), (2, 3)), ((5, 6, 7), (5, 4)))
-LAST_TURN = 4
+PAIRED = 4
 LAST_EXPERT = range(GROUPS - C // P, GROUPS)
 
 F32 = mybir.dt.float32
@@ -123,7 +124,7 @@ def tile_moe_duo_relu2_kernel(
                 nc.vector.tensor_copy(gathered[side][sort][:, columns(sort, groups)], windows[sort].indirect(offsets))
 
         gathers_behind = {}
-        for sort, pieces in ((WORDS, RUNS), (SCALES, SCALE_PIECES)):
+        for sort, pieces in ((WORDS, WORD_PIECES), (SCALES, SCALE_PIECES)):
             for groups in pieces:
                 taken = [PLACE[sort][j] for j in groups]
                 holder = max([-1] + [j for j in range(groups[0]) if PLACE[sort][j] in taken])
@@ -135,6 +136,8 @@ def tile_moe_duo_relu2_kernel(
         last_bank = banks[5]
 
         hb = keep.tile([P, S, PACK], BF16, name="hb", align_bytes=64)
+        squares = keep.tile([P, H], BF16, name="squares", align_bytes=64)
+        hb_pairs = keep.tile([P, 2 * P], F32, name="hb_pairs", align_bytes=64)
         relu_of = {}
 
         def last_sum(j):
@@ -174,18 +177,27 @@ def tile_moe_duo_relu2_kernel(
 
         def relu(j):
             pos_part = ring.tile([P, PACK, P], F32, name="pos_part", align_bytes=64)
-            src = sum_bank[j][:].rearrange("s (p t) -> s t p", t=PACK)
-            nc.scalar.activation(pos_part[:], src, ACT.Relu)
+            if j == PAIRED:
+                src = sum_bank[j][:].rearrange("s (p u e) -> s u p e", u=2, e=2)
+                flat = pos_part[:].rearrange("s t p -> s (t p)")
+                nc.scalar.activation(flat.rearrange("s (u p e) -> s u p e", u=2, e=2), src, ACT.Relu)
+                nc.gpsimd.tensor_tensor(squares[:], flat, flat, ALU.mult)
+            else:
+                src = sum_bank[j][:].rearrange("s (p t) -> s t p", t=PACK)
+                nc.scalar.activation(pos_part[:], src, ACT.Relu)
             relu_of[j] = pos_part
 
         def turn(j):
             turned = turn_bank[j][:].rearrange("p (t s) -> p t s", t=PACK)
+            if j == PAIRED:
+                for u in range(2):
+                    nc.tensor.transpose(turned[:, u, :], squares[:].bitcast(F32)[:, u * P : (u + 1) * P], ident[:])
+                dst = hb_pairs[:].rearrange("p (s u) -> p s u", u=2)
+                nc.scalar.copy(dst, turned[:, 0:2, :].rearrange("p u s -> p s u"))
+                return
             for t in range(PACK):
                 nc.tensor.transpose(turned[:, t, :], relu_of[j][:, t, :], ident[:])
-            step = P // 2 if j == LAST_TURN else P
-            for s0 in range(0, P, step):
-                src = turned[:, :, s0 : s0 + step].rearrange("p t s -> p s t")
-                nc.scalar.activation(hb[:, j * P + s0 : j * P + s0 + step, :], src, ACT.Square)
+            nc.scalar.activation(hb[:, j * P : (j + 1) * P, :], turned.rearrange("p t s -> p s t"), ACT.Square)
 
         for piece in gathers_behind[-1]:
             gather(*piece)
@@ -217,7 +229,8 @@ def tile_moe_duo_relu2_kernel(
         y = keep.tile([P, S], F32, name="y", align_bytes=64)
 
         def quantize(a, b):
-            nc.vector.quantize_mx(hw[:, a:b].bitcast(FP8X4), hs[:, a:b], hb[:, a:b, :].rearrange("p s t -> p (s t)"))
+            src = hb_pairs[:].bitcast(BF16) if a == PAIRED * P else hb[:, a:b, :].rearrange("p s t -> p (s t)")
+            nc.vector.quantize_mx(hw[:, a:b].bitcast(FP8X4), hs[:, a:b], src)
 
         def second_layer(bank, base, a, b):
             e = a // C
@@ -238,15 +251,15 @@ def tile_moe_duo_relu2_kernel(
         second_layer(bank_first, 0, 0, C)
         second_layer(bank_first, 0, C, mid)
         quantize(third, S)
-        second_layer(bank_mid, late, third, S)
+        second_layer(bank_mid, third, third, S)
         quantize(late, third)
-        second_layer(bank_mid, late, late, third)
-        quantize(mid, mid + P // 2)
-        quantize(mid + P // 2, late)
+        second_layer(banks[2], late, late, third)
+        quantize(mid, late)
         second_layer(last_bank, mid, mid, late)
         nc.scalar.copy(y[:, 0:mid], bank_first[:])
-        nc.vector.tensor_copy(y[:, late:S], bank_mid[:, 0 : S - late])
-        nc.scalar.copy(y[:, mid:late], last_bank[:, 0:P])
+        nc.scalar.copy(y[:, third:S], bank_mid[:, 0:C])
+        nc.scalar.copy(y[:, late:third], banks[2][:, 0:P])
+        nc.vector.tensor_copy(y[:, mid:late], last_bank[:, 0:P])
 
         part1 = keep.tile([P, T], F32, name="part1", align_bytes=64)
         part2 = keep.tile([P, T], F32, name="part2", align_bytes=64)

@@ -14,15 +14,27 @@ LIST_ROWS = 16
 TOKENS, PARTNERS = 0, 1
 WORDS, SCALES = 0, 1
 
-RUN = 3
-RUNS = [range(j, min(j + RUN, GROUPS)) for j in range(0, GROUPS, RUN)]
-SCALE_PIECES = [range(0, 2), range(2, 4), range(4, 6), range(6, 8)]
-WORD_PIECES = [range(0, 3), range(3, 5), range(5, 7), range(7, 8)]
-PLACES = 4
-PLACE = ((1, 2, 3, 0, 1, 2, 3, 1), (0, 1, 2, 3, 0, 1, 2, 3))
-STEPS = (((0, 1, 2), (0, 1)), ((3, 4), (2, 3)), ((5, 6, 7), (5, 4)))
+SUM, TURN = 0, 1
+
+DIRECT = range(GROUPS - C // P, GROUPS)
 PAIRED = 4
-LAST_EXPERT = range(GROUPS - C // P, GROUPS)
+WORD_PIECES = [range(0, 3)] + [range(j, min(j + 2, GROUPS)) for j in range(3, GROUPS, 2)]
+SCALE_PIECES = [range(j, j + 2) for j in range(0, GROUPS, 2)]
+PLACES = 4
+PLACE = ([(j + 1) % PLACES for j in range(GROUPS - 1)] + [1], [j % PLACES for j in range(GROUPS)])
+RUNS = (((0, 1, 2), (0, 1)), ((3, 4), (2, 3)), ((5, 6, 7), (5, PAIRED)))
+BANK_FROM = {
+    (SUM, 3): (SUM, 2),
+    (SUM, 4): (TURN, 0),
+    (TURN, 2): (TURN, 1),
+    (TURN, 3): (SUM, 0),
+    (SUM, 5): (SUM, 4),
+    (SUM, 6): (TURN, 2),
+    (SUM, 7): (TURN, 3),
+    (TURN, 5): (SUM, 1),
+    (TURN, 4): (SUM, 5),
+}
+WARM_UPS = 4
 
 F32 = mybir.dt.float32
 BF16 = mybir.dt.bfloat16
@@ -42,7 +54,7 @@ def tile_moe_duo_relu2_kernel(
     nc = tc.nc
     with ExitStack() as ctx:
         keep = ctx.enter_context(tc.tile_pool(name="keep", bufs=1))
-        ring = ctx.enter_context(tc.tile_pool(name="ring", bufs=RUN + 2))
+        ring = ctx.enter_context(tc.tile_pool(name="ring", bufs=5))
         ps_keep = ctx.enter_context(tc.psum_pool(name="ps_keep", bufs=1))
 
         tok_list = keep.tile([P, S // LIST_ROWS], U16, name="tok_list")
@@ -52,7 +64,7 @@ def tile_moe_duo_relu2_kernel(
         xw = keep.tile([P, T], I32, name="xw", tag="xw", align_bytes=64)
         xs = keep.tile([P, T], U8, name="xs", tag="xs", align_bytes=64)
         w1w = keep.tile([P, E, 2 * H], U8, name="w1w", align_bytes=64)
-        wpw = keep.tile([P, E, 2 * H], U8, name="wpw", tag="wpw", align_bytes=64)
+        wpw = keep.tile([P, E, 2 * H], U8, name="wpw", align_bytes=64)
         w2w = keep.tile([P, E, 2 * N], U8, name="w2w", align_bytes=64)
         w1s_pad = keep.tile([P, E * H + 4], U8, name="w1s_pad", align_bytes=64)
         wps_pad = keep.tile([P, E * H + 4], U8, name="wps_pad", align_bytes=64)
@@ -95,15 +107,15 @@ def tile_moe_duo_relu2_kernel(
         nc.sync.dma_start(pos2_list[:], pos2)
         nc.sync.dma_start(gates[:], gate.rearrange("r p t -> p r t"))
 
-        last_w = [keep.tile([P, PACK, 2 * P], U8, name="last_w%d" % side, tag="last_w%d" % side, align_bytes=64) for side in (TOKENS, PARTNERS)]
-        last_s = [keep.tile([P, PACK, P], U8, name="last_s%d" % side, align_bytes=64) for side in (TOKENS, PARTNERS)]
-        for side, scale_tile in ((TOKENS, w1s), (PARTNERS, wps)):
-            nc.gpsimd.tensor_copy(last_s[side][:], scale_tile[:, (E - 1) * H : E * H].rearrange("k (p t) -> k t p", t=PACK))
-        for side, words in ((TOKENS, w1w), (PARTNERS, wpw)):
-            nc.gpsimd.tensor_copy(
-                last_w[side][:].rearrange("k t (p b) -> k t p b", b=2),
-                words[:, E - 1, :].rearrange("k (p t b) -> k t p b", t=PACK, b=2),
-            )
+        direct_w = [keep.tile([P, PACK, 2 * P], U8, name="direct_w%d" % side, align_bytes=64) for side in (TOKENS, PARTNERS)]
+        direct_s = [keep.tile([P, PACK, P], U8, name="direct_s%d" % side, align_bytes=64) for side in (TOKENS, PARTNERS)]
+        weights = ((w1w, w1s), (wpw, wps))
+        for side in (TOKENS, PARTNERS):
+            src = weights[side][SCALES][:, (E - 1) * H : E * H].rearrange("k (p t) -> k t p", t=PACK)
+            nc.gpsimd.tensor_copy(direct_s[side][:], src)
+        for side in (TOKENS, PARTNERS):
+            src = weights[side][WORDS][:, E - 1, :].rearrange("k (p t b) -> k t p b", t=PACK, b=2)
+            nc.gpsimd.tensor_copy(direct_w[side][:].rearrange("k t (p b) -> k t p b", b=2), src)
 
         tok_w = keep.tile([P, PLACES * P], U32, name="tok_w", align_bytes=64)
         par_w = keep.tile([P, PLACES * P], U32, name="par_w", align_bytes=64)
@@ -113,60 +125,44 @@ def tile_moe_duo_relu2_kernel(
         windows = (xw[:].bitcast(U32), xs[:])
         gathered = ((tok_w, tok_s), (par_w, par_s))
         lists = (tok_list, par_list)
-        weights = ((w1w, w1s), (wpw, wps))
 
         def columns(sort, groups):
             return slice(PLACE[sort][groups[0]] * P, (PLACE[sort][groups[-1]] + 1) * P)
 
+        def gather_side(side, sort, groups):
+            offsets = lists[side][:, groups[0] * P // LIST_ROWS : (groups[-1] + 1) * P // LIST_ROWS]
+            nc.vector.tensor_copy(gathered[side][sort][:, columns(sort, groups)], windows[sort].indirect(offsets))
+
         def gather(sort, groups):
             for side in (TOKENS, PARTNERS):
-                offsets = lists[side][:, groups[0] * P // LIST_ROWS : (groups[-1] + 1) * P // LIST_ROWS]
-                nc.vector.tensor_copy(gathered[side][sort][:, columns(sort, groups)], windows[sort].indirect(offsets))
+                gather_side(side, sort, groups)
 
         gathers_behind = {}
-        for sort, pieces in ((WORDS, WORD_PIECES), (SCALES, SCALE_PIECES)):
+        for sort, pieces in ((WORDS, WORD_PIECES[1:]), (SCALES, SCALE_PIECES)):
             for groups in pieces:
                 taken = [PLACE[sort][j] for j in groups]
                 holder = max([-1] + [j for j in range(groups[0]) if PLACE[sort][j] in taken])
                 gathers_behind.setdefault(holder, []).append((sort, groups))
 
-        banks = [ps_keep.tile([P, H], F32, name="bank%d" % i) for i in range(6)]
-        sum_bank = [banks[i] for i in (0, 1, 2, 2, 3, 3, 4, 0)]
-        turn_bank = [banks[i] for i in (3, 4, 4, 0, 3, 1)]
-        last_bank = banks[5]
+        bank_of = {}
+        for sums, turns in RUNS:
+            for key in [(SUM, j) for j in sums] + [(TURN, j) for j in turns]:
+                if key in BANK_FROM:
+                    bank_of[key] = bank_of[BANK_FROM[key]]
+                else:
+                    bank_of[key] = ps_keep.tile([P, H], F32, name="bank%d_%d" % key)
+        last_bank = ps_keep.tile([P, H], F32, name="last_bank")
 
         hb = keep.tile([P, S, PACK], BF16, name="hb", align_bytes=64)
         squares = keep.tile([P, H], BF16, name="squares", align_bytes=64)
         hb_pairs = keep.tile([P, 2 * P], F32, name="hb_pairs", align_bytes=64)
         relu_of = {}
 
-        def last_sum(j):
-            for side in (TOKENS, PARTNERS):
-                for t in range(PACK):
-                    nc.tensor.matmul_mx(
-                        sum_bank[j][:, t * P : (t + 1) * P],
-                        lhsT=last_w[side][:, t, :].bitcast(FP4X4),
-                        lhsT_scale=last_s[side][:, t, :],
-                        rhs=gathered[side][WORDS][:, columns(WORDS, [j])].bitcast(FP8X4),
-                        rhs_scale=gathered[side][SCALES][:, columns(SCALES, [j])],
-                        start=(side == TOKENS and t == 0),
-                        stop=(side == PARTNERS and t == PACK - 1),
-                    )
-
-        def relu_square(j):
-            pos_part = ring.tile([P, P, PACK], F32, name="pos_part", align_bytes=64)
-            src = sum_bank[j][:].rearrange("p (t s) -> p s t", t=PACK)
-            step = P // 2 if j == GROUPS - 1 else P
-            for s0 in range(0, P, step):
-                part = pos_part[:, s0 : s0 + step, :]
-                nc.scalar.activation(part, src[:, s0 : s0 + step, :], ACT.Relu)
-                nc.vector.tensor_tensor(hb[:, j * P + s0 : j * P + s0 + step, :], part, part, ALU.mult)
-
-        def first_sum(j):
+        def slots_stationary_sum(j):
             e = j * P // C
             for side in (TOKENS, PARTNERS):
                 nc.tensor.matmul_mx(
-                    sum_bank[j][:],
+                    bank_of[SUM, j][:],
                     lhsT=gathered[side][WORDS][:, columns(WORDS, [j])].bitcast(FP8X4),
                     lhsT_scale=gathered[side][SCALES][:, columns(SCALES, [j])],
                     rhs=weights[side][WORDS][:, e, :].bitcast(FP4X4),
@@ -175,33 +171,58 @@ def tile_moe_duo_relu2_kernel(
                     stop=(side == PARTNERS),
                 )
 
-        def relu(j):
+        def weights_stationary_sum(j):
+            for side in (TOKENS, PARTNERS):
+                for t in range(PACK):
+                    nc.tensor.matmul_mx(
+                        bank_of[SUM, j][:, t * P : (t + 1) * P],
+                        lhsT=direct_w[side][:, t, :].bitcast(FP4X4),
+                        lhsT_scale=direct_s[side][:, t, :],
+                        rhs=gathered[side][WORDS][:, columns(WORDS, [j])].bitcast(FP8X4),
+                        rhs_scale=gathered[side][SCALES][:, columns(SCALES, [j])],
+                        start=(side == TOKENS and t == 0),
+                        stop=(side == PARTNERS and t == PACK - 1),
+                    )
+
+        def relu_turned(j):
             pos_part = ring.tile([P, PACK, P], F32, name="pos_part", align_bytes=64)
-            if j == PAIRED:
-                src = sum_bank[j][:].rearrange("s (p u e) -> s u p e", u=2, e=2)
-                flat = pos_part[:].rearrange("s t p -> s (t p)")
-                nc.scalar.activation(flat.rearrange("s (u p e) -> s u p e", u=2, e=2), src, ACT.Relu)
-                nc.gpsimd.tensor_tensor(squares[:], flat, flat, ALU.mult)
-            else:
-                src = sum_bank[j][:].rearrange("s (p t) -> s t p", t=PACK)
-                nc.scalar.activation(pos_part[:], src, ACT.Relu)
+            nc.scalar.activation(pos_part[:], bank_of[SUM, j][:].rearrange("s (p t) -> s t p", t=PACK), ACT.Relu)
             relu_of[j] = pos_part
 
         def turn(j):
-            turned = turn_bank[j][:].rearrange("p (t s) -> p t s", t=PACK)
-            if j == PAIRED:
-                for u in range(2):
-                    nc.tensor.transpose(turned[:, u, :], squares[:].bitcast(F32)[:, u * P : (u + 1) * P], ident[:])
-                dst = hb_pairs[:].rearrange("p (s u) -> p s u", u=2)
-                nc.scalar.copy(dst, turned[:, 0:2, :].rearrange("p u s -> p s u"))
-                return
+            turned = bank_of[TURN, j][:].rearrange("p (t s) -> p t s", t=PACK)
             for t in range(PACK):
                 nc.tensor.transpose(turned[:, t, :], relu_of[j][:, t, :], ident[:])
             nc.scalar.activation(hb[:, j * P : (j + 1) * P, :], turned.rearrange("p t s -> p s t"), ACT.Square)
 
+        def relu_square_paired(j):
+            pos_part = ring.tile([P, H], F32, name="pos_part", align_bytes=64)
+            src = bank_of[SUM, j][:].rearrange("s (p u e) -> s u p e", u=2, e=2)
+            nc.scalar.activation(pos_part[:].rearrange("s (u p e) -> s u p e", u=2, e=2), src, ACT.Relu)
+            nc.gpsimd.tensor_tensor(squares[:], pos_part[:], pos_part[:], ALU.mult)
+
+        def turn_paired(j):
+            turned = bank_of[TURN, j][:, 0 : 2 * P].rearrange("p (u s) -> p u s", u=2)
+            for u in range(2):
+                nc.tensor.transpose(turned[:, u, :], squares[:].bitcast(F32)[:, u * P : (u + 1) * P], ident[:])
+            nc.scalar.copy(hb_pairs[:].rearrange("p (s u) -> p s u", u=2), turned.rearrange("p u s -> p s u"))
+
+        def relu_square_direct(j):
+            pos_part = ring.tile([P, P, PACK], F32, name="pos_part", align_bytes=64)
+            src = bank_of[SUM, j][:].rearrange("p (t s) -> p s t", t=PACK)
+            for s0 in (0, P // 2):
+                part = pos_part[:, s0 : s0 + P // 2, :]
+                nc.scalar.activation(part, src[:, s0 : s0 + P // 2, :], ACT.Relu)
+                nc.vector.tensor_tensor(hb[:, j * P + s0 : j * P + s0 + P // 2, :], part, part, ALU.mult)
+
+        first = WORD_PIECES[0]
+        gather_side(TOKENS, WORDS, first[:1])
+        gather_side(TOKENS, WORDS, first[1:])
+        gather_side(PARTNERS, WORDS, first)
         for piece in gathers_behind[-1]:
             gather(*piece)
-        for i in range(3):
+
+        for i in range(WARM_UPS):
             nc.tensor.matmul_mx(
                 last_bank[:],
                 lhsT=tok_w[:, columns(WORDS, [0])].bitcast(FP8X4),
@@ -211,18 +232,25 @@ def tile_moe_duo_relu2_kernel(
                 start=True,
                 stop=True,
             )
-        for sums, turns in STEPS:
+
+        for sums, turns in RUNS:
             for j in sums:
-                if j in LAST_EXPERT:
-                    last_sum(j)
-                    relu_square(j)
+                if j in DIRECT:
+                    weights_stationary_sum(j)
+                    relu_square_direct(j)
+                elif j == PAIRED:
+                    slots_stationary_sum(j)
+                    relu_square_paired(j)
                 else:
-                    first_sum(j)
-                    relu(j)
+                    slots_stationary_sum(j)
+                    relu_turned(j)
                 for piece in gathers_behind.get(j, ()):
                     gather(*piece)
             for j in turns:
-                turn(j)
+                if j == PAIRED:
+                    turn_paired(j)
+                else:
+                    turn(j)
 
         hw = keep.tile([P, S], U32, name="hw", tag="xw", align_bytes=64)
         hs = keep.tile([P, S], U8, name="hs", tag="xs", align_bytes=64)
@@ -244,22 +272,21 @@ def tile_moe_duo_relu2_kernel(
                 stop=True,
             )
 
-        mid, third = 2 * C, 3 * C
-        late = mid + P
-        bank_first, bank_mid = sum_bank[GROUPS - 1], sum_bank[GROUPS - 2]
+        mid, late, third = PAIRED * P, (PAIRED + 1) * P, DIRECT[0] * P
+        bank_first, bank_direct, bank_late = bank_of[SUM, 7], bank_of[SUM, 6], bank_of[SUM, 3]
         quantize(0, mid)
         second_layer(bank_first, 0, 0, C)
         second_layer(bank_first, 0, C, mid)
         quantize(third, S)
-        second_layer(bank_mid, third, third, S)
+        second_layer(bank_direct, third, third, S)
         quantize(late, third)
-        second_layer(banks[2], late, late, third)
+        second_layer(bank_late, late, late, third)
         quantize(mid, late)
         second_layer(last_bank, mid, mid, late)
         nc.scalar.copy(y[:, 0:mid], bank_first[:])
-        nc.scalar.copy(y[:, third:S], bank_mid[:, 0:C])
-        nc.scalar.copy(y[:, late:third], banks[2][:, 0:P])
-        nc.vector.tensor_copy(y[:, mid:late], last_bank[:, 0:P])
+        nc.vector.tensor_copy(y[:, third:S], bank_direct[:, 0:C])
+        nc.scalar.copy(y[:, late:third], bank_late[:, 0:P])
+        nc.scalar.copy(y[:, mid:late], last_bank[:, 0:P])
 
         part1 = keep.tile([P, T], F32, name="part1", align_bytes=64)
         part2 = keep.tile([P, T], F32, name="part2", align_bytes=64)

@@ -34,7 +34,7 @@ BANK_FROM = {
     (TURN, 5): (SUM, 1),
     (TURN, 4): (SUM, 5),
 }
-WARM_UPS = 4
+WARM_UPS = 3
 
 F32 = mybir.dt.float32
 BF16 = mybir.dt.bfloat16
@@ -129,16 +129,13 @@ def tile_moe_duo_relu2_kernel(
         def columns(sort, groups):
             return slice(PLACE[sort][groups[0]] * P, (PLACE[sort][groups[-1]] + 1) * P)
 
-        def gather_side(side, sort, groups):
-            offsets = lists[side][:, groups[0] * P // LIST_ROWS : (groups[-1] + 1) * P // LIST_ROWS]
-            nc.vector.tensor_copy(gathered[side][sort][:, columns(sort, groups)], windows[sort].indirect(offsets))
-
         def gather(sort, groups):
             for side in (TOKENS, PARTNERS):
-                gather_side(side, sort, groups)
+                offsets = lists[side][:, groups[0] * P // LIST_ROWS : (groups[-1] + 1) * P // LIST_ROWS]
+                nc.vector.tensor_copy(gathered[side][sort][:, columns(sort, groups)], windows[sort].indirect(offsets))
 
         gathers_behind = {}
-        for sort, pieces in ((WORDS, WORD_PIECES[1:]), (SCALES, SCALE_PIECES)):
+        for sort, pieces in ((WORDS, WORD_PIECES), (SCALES, SCALE_PIECES)):
             for groups in pieces:
                 taken = [PLACE[sort][j] for j in groups]
                 holder = max([-1] + [j for j in range(groups[0]) if PLACE[sort][j] in taken])
@@ -215,10 +212,6 @@ def tile_moe_duo_relu2_kernel(
                 nc.scalar.activation(part, src[:, s0 : s0 + P // 2, :], ACT.Relu)
                 nc.vector.tensor_tensor(hb[:, j * P + s0 : j * P + s0 + P // 2, :], part, part, ALU.mult)
 
-        first = WORD_PIECES[0]
-        gather_side(TOKENS, WORDS, first[:1])
-        gather_side(TOKENS, WORDS, first[1:])
-        gather_side(PARTNERS, WORDS, first)
         for piece in gathers_behind[-1]:
             gather(*piece)
 

from contextlib import ExitStack

import concourse.mybir as mybir
from concourse.masks import make_identity

K, T, E, C, H, N = 512, 512, 4, 256, 512, 128
S = E * C
P = 128
FLOPS = 2 * S * (2 * K * H + H * N)

GROUPS = S // P
PACK = 4
LIST_ROWS = 16
TOKENS, PARTNERS = 0, 1
WORDS, SCALES = 0, 1

SUM, TURN = 0, 1

DIRECT = range(GROUPS - C // P, GROUPS)
PAIRED = 4
WORD_PIECES = [range(0, 3)] + [range(j, min(j + 2, GROUPS)) for j in range(3, GROUPS, 2)]
SCALE_PIECES = [range(j, j + 2) for j in range(0, GROUPS, 2)]
PLACES = 4
PLACE = ([(j + 1) % PLACES for j in range(GROUPS - 1)] + [1], [j % PLACES for j in range(GROUPS)])
RUNS = (((0, 1, 2), (0, 1)), ((3, 4), (2, 3)), ((5, 6, 7), (5, PAIRED)))
BANK_FROM = {
    (SUM, 3): (SUM, 2),
    (SUM, 4): (TURN, 0),
    (TURN, 2): (TURN, 1),
    (TURN, 3): (SUM, 0),
    (SUM, 5): (SUM, 4),
    (SUM, 6): (TURN, 2),
    (SUM, 7): (TURN, 3),
    (TURN, 5): (SUM, 1),
    (TURN, 4): (SUM, 5),
}
WARM_UPS = 3

F32 = mybir.dt.float32
BF16 = mybir.dt.bfloat16
I32 = mybir.dt.int32
U32 = mybir.dt.uint32
U16 = mybir.dt.uint16
U8 = mybir.dt.uint8
FP8X4 = mybir.dt.float8_e4m3fn_x4
FP4X4 = mybir.dt.float4_e2m1fn_x4
ACT = mybir.ActivationFunctionType
ALU = mybir.AluOpType


def tile_moe_duo_relu2_kernel(
    tc, x_words, x_scales, w1_words, w1_scales, wp_words, wp_scales, w2_words, w2_scales, gate, offs, pos1, pos2, offs2, out
):
    nc = tc.nc
    with ExitStack() as ctx:
        keep = ctx.enter_context(tc.tile_pool(name="keep", bufs=1))
        ring = ctx.enter_context(tc.tile_pool(name="ring", bufs=5))
        ps_keep = ctx.enter_context(tc.psum_pool(name="ps_keep", bufs=1))

        tok_list = keep.tile([P, S // LIST_ROWS], U16, name="tok_list")
        par_list = keep.tile([P, S // LIST_ROWS], U16, name="par_list")
        pos1_list = keep.tile([P, T // LIST_ROWS], U16, name="pos1_list")
        pos2_list = keep.tile([P, T // LIST_ROWS], U16, name="pos2_list")
        xw = keep.tile([P, T], I32, name="xw", tag="xw", align_bytes=64)
        xs = keep.tile([P, T], U8, name="xs", tag="xs", align_bytes=64)
        w1w = keep.tile([P, E, 2 * H], U8, name="w1w", align_bytes=64)
        wpw = keep.tile([P, E, 2 * H], U8, name="wpw", align_bytes=64)
        w2w = keep.tile([P, E, 2 * N], U8, name="w2w", align_bytes=64)
        w1s_pad = keep.tile([P, E * H + 4], U8, name="w1s_pad", align_bytes=64)
        wps_pad = keep.tile([P, E * H + 4], U8, name="wps_pad", align_bytes=64)
        w2s_pad = keep.tile([P, E * N + 4], U8, name="w2s_pad", align_bytes=64)
        gates = keep.tile([P, 2, T], F32, name="gates", align_bytes=64)
        ident = keep.tile([P, P], F32, name="ident", align_bytes=64)

        w1s = w1s_pad[:, 0 : E * H]
        wps = wps_pad[:, 0 : E * H]
        w2s = w2s_pad[:, 0 : E * N]
        for scale_tile in (xs, w1s_pad, wps_pad, w2s_pad):
            nc.vector.memset(scale_tile[:].bitcast(I32), 0)

        def load_scales(scale_tile, src):
            by_row = src.rearrange("e s (q r) c -> r q (e s) c", r=PACK)
            for r in range(PACK):
                dst = scale_tile[r:P:32, :].bitcast(I32).rearrange("q (e c) -> q e c", e=E)
                nc.sync.dma_start(dst, by_row[r].bitcast(I32))

        def load_words(queue, tile, src, e0, e1):
            queue.dma_start(tile[:, e0:e1, :].bitcast(I32), src[e0:e1, 0].rearrange("e p c -> p e c").bitcast(I32))

        nc.sync.dma_start(xw[:], x_words[0].rearrange("p t d -> p (t d)").bitcast(I32))
        nc.sync.dma_start(tok_list[:], offs)
        load_words(nc.gpsimd, wpw, wp_words, 0, 1)
        nc.sync.dma_start(par_list[:], offs2)
        xs_rows = x_scales[0].rearrange("(q r) c -> r q c", r=PACK)
        for r in range(PACK):
            nc.scalar.dma_start(xs[r:P:32, :].bitcast(I32), xs_rows[r].bitcast(I32))
        load_words(nc.sync, w1w, w1_words, 0, 1)
        make_identity(nc, ident[:])
        load_scales(wps, wp_scales)
        load_scales(w1s, w1_scales)
        for e0, e1 in ((1, E - 1), (E - 1, E)):
            load_words(nc.sync, w1w, w1_words, e0, e1)
            load_words(nc.sync, wpw, wp_words, e0, e1)
        load_words(nc.sync, w2w, w2_words, 0, E)
        load_scales(w2s, w2_scales)
        nc.sync.dma_start(pos1_list[:], pos1)
        nc.sync.dma_start(pos2_list[:], pos2)
        nc.sync.dma_start(gates[:], gate.rearrange("r p t -> p r t"))

        direct_w = [keep.tile([P, PACK, 2 * P], U8, name="direct_w%d" % side, align_bytes=64) for side in (TOKENS, PARTNERS)]
        direct_s = [keep.tile([P, PACK, P], U8, name="direct_s%d" % side, align_bytes=64) for side in (TOKENS, PARTNERS)]
        weights = ((w1w, w1s), (wpw, wps))
        for side in (TOKENS, PARTNERS):
            src = weights[side][SCALES][:, (E - 1) * H : E * H].rearrange("k (p t) -> k t p", t=PACK)
            nc.gpsimd.tensor_copy(direct_s[side][:], src)
        for side in (TOKENS, PARTNERS):
            src = weights[side][WORDS][:, E - 1, :].rearrange("k (p t b) -> k t p b", t=PACK, b=2)
            nc.gpsimd.tensor_copy(direct_w[side][:].rearrange("k t (p b) -> k t p b", b=2), src)

        tok_w = keep.tile([P, PLACES * P], U32, name="tok_w", align_bytes=64)
        par_w = keep.tile([P, PLACES * P], U32, name="par_w", align_bytes=64)
        tok_s = keep.tile([P, PLACES * P], U8, name="tok_s", align_bytes=64)
        par_s = keep.tile([P, PLACES * P], U8, name="par_s", align_bytes=64)

        windows = (xw[:].bitcast(U32), xs[:])
        gathered = ((tok_w, tok_s), (par_w, par_s))
        lists = (tok_list, par_list)

        def columns(sort, groups):
            return slice(PLACE[sort][groups[0]] * P, (PLACE[sort][groups[-1]] + 1) * P)

        def gather(sort, groups):
            for side in (TOKENS, PARTNERS):
                offsets = lists[side][:, groups[0] * P // LIST_ROWS : (groups[-1] + 1) * P // LIST_ROWS]
                nc.vector.tensor_copy(gathered[side][sort][:, columns(sort, groups)], windows[sort].indirect(offsets))

        gathers_behind = {}
        for sort, pieces in ((WORDS, WORD_PIECES), (SCALES, SCALE_PIECES)):
            for groups in pieces:
                taken = [PLACE[sort][j] for j in groups]
                holder = max([-1] + [j for j in range(groups[0]) if PLACE[sort][j] in taken])
                gathers_behind.setdefault(holder, []).append((sort, groups))

        bank_of = {}
        for sums, turns in RUNS:
            for key in [(SUM, j) for j in sums] + [(TURN, j) for j in turns]:
                if key in BANK_FROM:
                    bank_of[key] = bank_of[BANK_FROM[key]]
                else:
                    bank_of[key] = ps_keep.tile([P, H], F32, name="bank%d_%d" % key)
        last_bank = ps_keep.tile([P, H], F32, name="last_bank")

        hb = keep.tile([P, S, PACK], BF16, name="hb", align_bytes=64)
        squares = keep.tile([P, H], BF16, name="squares", align_bytes=64)
        hb_pairs = keep.tile([P, 2 * P], F32, name="hb_pairs", align_bytes=64)
        relu_of = {}

        def slots_stationary_sum(j):
            e = j * P // C
            for side in (TOKENS, PARTNERS):
                nc.tensor.matmul_mx(
                    bank_of[SUM, j][:],
                    lhsT=gathered[side][WORDS][:, columns(WORDS, [j])].bitcast(FP8X4),
                    lhsT_scale=gathered[side][SCALES][:, columns(SCALES, [j])],
                    rhs=weights[side][WORDS][:, e, :].bitcast(FP4X4),
                    rhs_scale=weights[side][SCALES][:, e * H : (e + 1) * H],
                    start=(side == TOKENS),
                    stop=(side == PARTNERS),
                )

        def weights_stationary_sum(j):
            for side in (TOKENS, PARTNERS):
                for t in range(PACK):
                    nc.tensor.matmul_mx(
                        bank_of[SUM, j][:, t * P : (t + 1) * P],
                        lhsT=direct_w[side][:, t, :].bitcast(FP4X4),
                        lhsT_scale=direct_s[side][:, t, :],
                        rhs=gathered[side][WORDS][:, columns(WORDS, [j])].bitcast(FP8X4),
                        rhs_scale=gathered[side][SCALES][:, columns(SCALES, [j])],
                        start=(side == TOKENS and t == 0),
                        stop=(side == PARTNERS and t == PACK - 1),
                    )

        def relu_turned(j):
            pos_part = ring.tile([P, PACK, P], F32, name="pos_part", align_bytes=64)
            nc.scalar.activation(pos_part[:], bank_of[SUM, j][:].rearrange("s (p t) -> s t p", t=PACK), ACT.Relu)
            relu_of[j] = pos_part

        def turn(j):
            turned = bank_of[TURN, j][:].rearrange("p (t s) -> p t s", t=PACK)
            for t in range(PACK):
                nc.tensor.transpose(turned[:, t, :], relu_of[j][:, t, :], ident[:])
            nc.scalar.activation(hb[:, j * P : (j + 1) * P, :], turned.rearrange("p t s -> p s t"), ACT.Square)

        def relu_square_paired(j):
            pos_part = ring.tile([P, H], F32, name="pos_part", align_bytes=64)
            src = bank_of[SUM, j][:].rearrange("s (p u e) -> s u p e", u=2, e=2)
            nc.scalar.activation(pos_part[:].rearrange("s (u p e) -> s u p e", u=2, e=2), src, ACT.Relu)
            nc.gpsimd.tensor_tensor(squares[:], pos_part[:], pos_part[:], ALU.mult)

        def turn_paired(j):
            turned = bank_of[TURN, j][:, 0 : 2 * P].rearrange("p (u s) -> p u s", u=2)
            for u in range(2):
                nc.tensor.transpose(turned[:, u, :], squares[:].bitcast(F32)[:, u * P : (u + 1) * P], ident[:])
            nc.scalar.copy(hb_pairs[:].rearrange("p (s u) -> p s u", u=2), turned.rearrange("p u s -> p s u"))

        def relu_square_direct(j):
            pos_part = ring.tile([P, P, PACK], F32, name="pos_part", align_bytes=64)
            src = bank_of[SUM, j][:].rearrange("p (t s) -> p s t", t=PACK)
            for s0 in (0, P // 2):
                part = pos_part[:, s0 : s0 + P // 2, :]
                nc.scalar.activation(part, src[:, s0 : s0 + P // 2, :], ACT.Relu)
                nc.vector.tensor_tensor(hb[:, j * P + s0 : j * P + s0 + P // 2, :], part, part, ALU.mult)

        for piece in gathers_behind[-1]:
            gather(*piece)

        for i in range(WARM_UPS):
            nc.tensor.matmul_mx(
                last_bank[:],
                lhsT=tok_w[:, columns(WORDS, [0])].bitcast(FP8X4),
                lhsT_scale=w1w[:, 0, 0:P],
                rhs=w1w[:, 0, :].bitcast(FP4X4),
                rhs_scale=w1w[:, 0, 0:H],
                start=True,
                stop=True,
            )

        for sums, turns in RUNS:
            for j in sums:
                if j in DIRECT:
                    weights_stationary_sum(j)
                    relu_square_direct(j)
                elif j == PAIRED:
                    slots_stationary_sum(j)
                    relu_square_paired(j)
                else:
                    slots_stationary_sum(j)
                    relu_turned(j)
                for piece in gathers_behind.get(j, ()):
                    gather(*piece)
            for j in turns:
                if j == PAIRED:
                    turn_paired(j)
                else:
                    turn(j)

        hw = keep.tile([P, S], U32, name="hw", tag="xw", align_bytes=64)
        hs = keep.tile([P, S], U8, name="hs", tag="xs", align_bytes=64)
        y = keep.tile([P, S], F32, name="y", align_bytes=64)

        def quantize(a, b):
            src = hb_pairs[:].bitcast(BF16) if a == PAIRED * P else hb[:, a:b, :].rearrange("p s t -> p (s t)")
            nc.vector.quantize_mx(hw[:, a:b].bitcast(FP8X4), hs[:, a:b], src)

        def second_layer(bank, base, a, b):
            e = a // C
            nc.tensor.matmul_mx(
                bank[:, a - base : b - base],
                lhsT=w2w[:, e, :].bitcast(FP4X4),
                lhsT_scale=w2s[:, e * N : (e + 1) * N],
                rhs=hw[:, a:b].bitcast(FP8X4),
                rhs_scale=hs[:, a:b],
                start=True,
                stop=True,
            )

        mid, late, third = PAIRED * P, (PAIRED + 1) * P, DIRECT[0] * P
        bank_first, bank_direct, bank_late = bank_of[SUM, 7], bank_of[SUM, 6], bank_of[SUM, 3]
        quantize(0, mid)
        second_layer(bank_first, 0, 0, C)
        second_layer(bank_first, 0, C, mid)
        quantize(third, S)
        second_layer(bank_direct, third, third, S)
        quantize(late, third)
        second_layer(bank_late, late, late, third)
        quantize(mid, late)
        second_layer(last_bank, mid, mid, late)
        nc.scalar.copy(y[:, 0:mid], bank_first[:])
        nc.vector.tensor_copy(y[:, third:S], bank_direct[:, 0:C])
        nc.scalar.copy(y[:, late:third], bank_late[:, 0:P])
        nc.scalar.copy(y[:, mid:late], last_bank[:, 0:P])

        part1 = keep.tile([P, T], F32, name="part1", align_bytes=64)
        part2 = keep.tile([P, T], F32, name="part2", align_bytes=64)
        res = keep.tile([P, T], F32, name="res", align_bytes=64)

        def weigh(dst, lst, r, a, b):
            offsets = lst[:, a // LIST_ROWS : b // LIST_ROWS]
            nc.vector.tensor_tensor(dst[:, a:b], y[:].indirect(offsets), gates[:, r, a:b], ALU.mult)

        def finish(a, b):
            nc.vector.tensor_tensor(res[:, a:b], part1[:, a:b], part2[:, a:b], ALU.add)
            nc.sync.dma_start(out[:, a:b], res[:, a:b])

        half = T // 2
        weigh(part1, pos1_list, 0, 0, T)
        weigh(part2, pos2_list, 1, 0, half)
        weigh(part2, pos2_list, 1, half, T)
        finish(0, half)
        finish(half, T)
